import numpy as np
import ml_dtypes


def mxq(x, axis, fmt="e4m3"):
    dtype, down = {"e4m3": (ml_dtypes.float8_e4m3fn, 7), "e5m2": (ml_dtypes.float8_e5m2, 14)}[fmt]
    v = np.moveaxis(np.asarray(x, np.float32).astype(ml_dtypes.bfloat16).astype(np.float64), axis, -1)
    blocks = v.reshape(v.shape[:-1] + (-1, 32))
    amax = np.abs(blocks).max(-1, keepdims=True)
    byte = np.maximum(np.where(amax > 0, np.frexp(amax)[1] - 1 + 127, 0) - down, 1)
    scale = np.exp2(byte - 127.0)
    codes = (blocks / scale).astype(np.float32).astype(dtype).astype(np.float64)
    return np.moveaxis((codes * scale).reshape(v.shape), -1, axis)


WIDE = False


def mx_kscale(k):
    if not WIDE:
        return np.ones(k)
    levels = np.array([10, -10, 5, -5, 0])
    if k % 512:
        return np.exp2(np.random.permutation(np.resize(levels, k // 32))).repeat(32)
    a = np.empty((k // 512, 16))
    for p in range(k // 512):
        a[p, :8] = np.random.permutation(np.resize(levels, 8))
        for g in range(8):
            far = levels[np.abs(levels - a[p, g]) >= 10]
            a[p, g + 8] = far[np.random.randint(len(far))]
    return np.exp2(a.ravel()).repeat(32)


def f64(x):
    return np.asarray(x).astype(np.float64)


def striped(idx):
    return np.tile(idx.reshape(-1, 16).T, (8, 1)).astype(np.uint16)


def unstriped(offs):
    return offs[:16].T.reshape(-1).astype(np.int64)


E2M1 = np.array([0.0, 0.5, 1.0, 1.5, 2.0, 3.0, 4.0, 6.0, -0.0, -0.5, -1.0, -1.5, -2.0, -3.0, -4.0, -6.0])


def pack_weight(w, fmt):
    k, n = w.shape
    w = f64(np.asarray(w, np.float32).astype(ml_dtypes.bfloat16)).reshape(k // 32, 32, n)
    amax = np.abs(w).max(1)
    if fmt == "e4m3":
        byte = np.frexp(amax)[1] - 1 + 127 - 7
    else:
        mant, ex = np.frexp(amax / 6.0)
        byte = np.where(mant > 0.5, ex, ex - 1) + 127
    byte = np.clip(np.where(amax > 0, byte, 1), 1, 254)
    scaled = (w * np.exp2(127.0 - byte)[:, None, :]).reshape(k, n).astype(np.float32)
    by_word = np.ascontiguousarray(scaled.reshape(k // 512, 128, 4, n).transpose(0, 1, 3, 2))
    if fmt == "e4m3":
        words = by_word.astype(ml_dtypes.float8_e4m3fn).view(np.uint8)
    else:
        c = by_word.astype(ml_dtypes.float4_e2m1fn).view(np.uint8) & 0xF
        words = (c[..., 0::2] | (c[..., 1::2] << 4)).reshape(k // 512, 128, 2 * n)
    return np.ascontiguousarray(words), np.ascontiguousarray(byte.astype(np.uint8).reshape(k // 512, 16, n))


def unpack_weight(words, scales, fmt):
    g, _, n = scales.shape
    words = np.ascontiguousarray(words).reshape(g, 128, n, -1)
    if fmt == "e4m3":
        vals = words.view(ml_dtypes.float8_e4m3fn).astype(np.float64)
    else:
        nib = np.empty((g, 128, n, 4), np.uint8)
        nib[..., 0::2] = words & 0xF
        nib[..., 1::2] = words >> 4
        vals = E2M1[nib]
    vals = vals * np.repeat(np.exp2(scales.astype(np.float64) - 127.0), 8, axis=1)[..., None]
    return vals.transpose(0, 1, 3, 2).reshape(g * 512, n)


def gelu(v):
    return 0.5 * v * (1.0 + np.tanh(np.sqrt(2.0 / np.pi) * (v + 0.044715 * v**3)))


K, H, T, S, T2, S2 = 1536, 512, 4096, 1024, 2048, 1024


def setup_inputs():
    n = np.random.standard_normal
    s = mx_kscale(K)[:, None]
    u = mx_kscale(H)[:, None]
    w = mx_kscale(S2)[:, None]
    tab_words, tab_scales = pack_weight(n((K, T)) * s, "e4m3")
    tab2_words, tab2_scales = pack_weight(1.5 * n((H, T2)) / np.sqrt(H) / u, "e4m3")
    vm_words, vm_scales = pack_weight(1.5 * n((S2, H)) / np.sqrt(S2) / w, "e2m1")
    return {
        "tab_words": tab_words, "tab_scales": tab_scales,
        "offs": striped(np.random.permutation(T)[:S]),
        "tab2_words": tab2_words, "tab2_scales": tab2_scales,
        "offs2": striped(np.random.permutation(T2)[:S2]),
        "wq": (n((K, H)) / np.sqrt(K) / s * u.T).astype(np.float32),
        "bq": (0.3 * n(H) * u[:, 0]).astype(np.float32),
        "pw": (np.exp(0.3 * n(S2)) * w[:, 0]).astype(np.float32),
        "vm_words": vm_words, "vm_scales": vm_scales,
        "rg": (np.random.uniform(0.5, 1.5, H) / u[:, 0]).astype(np.float32),
    }


def reference(tab_words, tab_scales, offs, tab2_words, tab2_scales, offs2, wq, bq, pw, vm_words, vm_scales, rg):
    v = unpack_weight(tab_words, tab_scales, "e4m3")[:, unstriped(offs)]
    v2 = unpack_weight(tab2_words, tab2_scales, "e4m3")[:, unstriped(offs2)]
    vm = unpack_weight(vm_words, vm_scales, "e2m1")
    h = (mxq(f64(wq), 0, "e4m3").T @ v) + f64(bq)[:, None]
    e = v2.T @ mxq(h, 0, "e4m3")
    d = f64(pw)[:, None] * (1.0 / (1.0 + np.exp(-e)))
    x = vm.T @ mxq(d, 0, "e4m3")
    out = f64(rg)[:, None] * h + x
    return out

@@ -1,0 +1,292 @@
+from contextlib import ExitStack
+
+import concourse.mybir as mybir
+
+K, H, T, S, T2, S2 = 1536, 512, 4096, 1024, 2048, 1024
+FLOPS = 2 * S * (K * H + H * S2 + S2 * H)
+
+F32 = mybir.dt.float32
+BF16 = mybir.dt.bfloat16
+I32 = mybir.dt.int32
+U32 = mybir.dt.uint32
+U16 = mybir.dt.uint16
+U8 = mybir.dt.uint8
+FP8X4 = mybir.dt.float8_e4m3fn_x4
+FP4X4 = mybir.dt.float4_e2m1fn_x4
+ACT = mybir.ActivationFunctionType
+ALU = mybir.AluOpType
+
+P = 128
+PACK = 4
+KP = P * PACK
+PASSES = K // KP
+MB = S2 // KP
+SUB = 128
+NSUB = S // SUB
+H_WIDTHS = (128, 128, 256, 256, 256)
+IL_ON_VECTOR = 3
+
+
+def tile_list_prior_art_expansion_kernel(
+    tc, tab_words, tab_scales, offs, tab2_words, tab2_scales, offs2, wq, bq, pw, vm_words, vm_scales, rg, out
+):
+    nc = tc.nc
+    with ExitStack() as ctx:
+        keep = ctx.enter_context(tc.tile_pool(name="keep", bufs=1))
+        psum = ctx.enter_context(tc.psum_pool(name="psum", bufs=1))
+
+        def sb(name, shape, dtype):
+            return keep.tile(shape, dtype, name=name, align_bytes=64)
+
+        def bank(k, name):
+            return psum.tile([P, KP], F32, name=name, tag="bank%d" % k)
+
+        list1 = keep.tile([P, S // 16], U16, name="list1")
+        list2 = keep.tile([P, S2 // 16], U16, name="list2")
+        t2_words = sb("t2_words", [P, T2], I32)
+        t2_scales = sb("t2_scales", [P, T2], U8)
+        t_words = [sb("t_words%d" % a, [P, T], I32) for a in range(PASSES)]
+        t_scales = sb("t_scales", [P, T], U8)
+        w_raw = [sb("w_raw%d" % a, [P, PACK, H], F32) for a in range(PASSES)]
+        vm_raw = sb("vm_raw", [P, MB, H // 2], I32)
+        vm_raw_scales = sb("vm_raw_scales", [P, MB * H], U8)
+        bq_t = sb("bq_t", [P, PACK], F32)
+        rg_t = sb("rg_t", [P, PACK], F32)
+        pw_t = sb("pw_t", [P, MB, PACK], F32)
+        warm = sb("warm", [P, 2], F32)
+
+        nc.vector.memset(t2_scales[:].bitcast(I32), 0)
+        nc.gpsimd.memset(t_scales[:].bitcast(I32), 0)
+        nc.vector.memset(vm_raw_scales[:].bitcast(I32), 0)
+        nc.vector.memset(warm[:, 0:1], 0.0)
+        nc.scalar.activation(warm[:, 1:2], warm[:, 0:1], ACT.Sigmoid)
+
+        def words_of(src, a):
+            return src[a].rearrange("p n i -> p (n i)").bitcast(I32)
+
+        def load_w(a):
+            nc.sync.dma_start(w_raw[a][:], wq[a * KP : (a + 1) * KP, :].rearrange("(p i) r -> p i r", i=PACK))
+
+        nc.sync.dma_start(list2[:], offs2)
+        nc.sync.dma_start(t2_words[:], words_of(tab2_words, 0))
+        for q in range(4):
+            nc.sync.dma_start(t2_scales[32 * q : 32 * q + 4, :].bitcast(I32), tab2_scales[0, 4 * q : 4 * q + 4, :].bitcast(I32))
+        nc.sync.dma_start(list1[:], offs)
+        nc.sync.dma_start(t_words[0][:], words_of(tab_words, 0))
+        load_w(0)
+        nc.sync.dma_start(bq_t[:], bq.rearrange("(p t) -> p t", t=PACK))
+        nc.sync.dma_start(pw_t[:], pw.rearrange("(b p t) -> p b t", b=MB, t=PACK))
+        nc.sync.dma_start(rg_t[:], rg.rearrange("(p t) -> p t", t=PACK))
+        nc.sync.dma_start(vm_raw[:], vm_words.rearrange("b p n -> p b n").bitcast(I32))
+        load_w(1)
+        for q in range(4):
+            nc.sync.dma_start(
+                vm_raw_scales[32 * q : 32 * q + 4, :].bitcast(I32).rearrange("r (b n) -> r b n", b=MB),
+                vm_scales[:, 4 * q : 4 * q + 4, :].rearrange("b r n -> r b n").bitcast(I32),
+            )
+        load_w(2)
+        for a in range(1, PASSES):
+            nc.sync.dma_start(t_words[a][:], words_of(tab_words, a))
+
+        for q in range(4):
+            nc.gpsimd.dma_start(
+                t_scales[32 * q : 32 * q + 4 * PASSES, :].bitcast(I32), tab_scales[:, 4 * q : 4 * q + 4, :].bitcast(I32)
+            )
+
+        def deal(dst, src):
+            nc.vector.tensor_copy(
+                dst.rearrange("p (b t m) -> p b m t", b=MB, t=PACK), src.rearrange("p (b m t) -> p b m t", b=MB, t=PACK)
+            )
+
+        v2_picked = sb("v2_picked", [P, S2], U32)
+        v2_picked_scales = sb("v2_picked_scales", [P, S2], U8)
+        v2_codes = sb("v2_codes", [P, S2], U32)
+        v2_scales = sb("v2_scales", [P, S2], U8)
+        nc.vector.tensor_copy(v2_picked[:], t2_words[:].bitcast(U32).indirect(list2[:]))
+        nc.vector.tensor_copy(v2_picked_scales[:], t2_scales[:].indirect(list2[:]))
+        deal(v2_codes[:], v2_picked[:])
+        deal(v2_scales[:], v2_picked_scales[:])
+
+        v_codes = [sb("v_codes%d" % a, [P, S], U32) for a in range(PASSES)]
+        v_scales = sb("v_scales", [P, S], U8)
+
+        def gather_words(a, j0, j1):
+            nc.vector.tensor_copy(v_codes[a][:, j0:j1], t_words[a][:].bitcast(U32).indirect(list1[:, j0 // 16 : j1 // 16]))
+
+        w_codes = [sb("w_codes%d" % a, [P, H], U32) for a in range(PASSES)]
+        w_scales = [sb("w_scales%d" % a, [P, H], U8) for a in range(PASSES)]
+        w_bf = [sb("w_bf%d" % a, [P, H * PACK], BF16) for a in range(PASSES)]
+        for a in range(PASSES):
+            nc.scalar.copy(
+                w_bf[a][:].rearrange("p (t m i) -> p m i t", t=PACK, i=PACK),
+                w_raw[a][:].rearrange("p i (m t) -> p m i t", t=PACK),
+            )
+
+        def quantize_w(a):
+            nc.vector.quantize_mx(w_codes[a][:].bitcast(FP8X4), w_scales[a][:], w_bf[a][:])
+
+        vm_codes = sb("vm_codes", [P, MB * H * 2], U8)
+        vm_scale = sb("vm_scale", [P, MB * H], U8)
+
+        gather_words(0, 0, S)
+        nc.vector.tensor_copy(v_scales[:], t_scales[:].indirect(list1[:]))
+        quantize_w(0)
+        deal(vm_codes[:].bitcast(U16), vm_raw[:].rearrange("p b n -> p (b n)").bitcast(U16))
+        quantize_w(1)
+        deal(vm_scale[:], vm_raw_scales[:])
+        quantize_w(2)
+        gather_words(1, 0, S // 2)
+        gather_words(1, S // 2, S)
+
+        starts = [sum(H_WIDTHS[:c]) for c in range(len(H_WIDTHS))]
+        h_banks = []
+        nb = 0
+        for c, w in enumerate(H_WIDTHS):
+            n = w // SUB
+            h_banks.append([bank(nb + u, "h_bank%d_%d" % (c, u)) for u in range(n)])
+            nb = nb + n
+
+        def h_psum(c, t):
+            w = H_WIDTHS[c]
+            per = KP // w
+            return h_banks[c][t // per][:, (t % per) * w : (t % per + 1) * w]
+
+        def first_product(c, a):
+            w = H_WIDTHS[c]
+            per = KP // w
+            cols = slice(starts[c], starts[c] + w)
+            for t in range(PACK):
+                nc.tensor.matmul_mx(
+                    h_psum(c, t),
+                    lhsT=w_codes[a][:, t * P : (t + 1) * P].bitcast(FP8X4),
+                    lhsT_scale=w_scales[a][:, t * P : (t + 1) * P],
+                    rhs=v_codes[a][:, cols].bitcast(FP8X4),
+                    rhs_scale=v_scales[4 * a : P, cols],
+                    start=(a == 0 and t % per == 0),
+                    stop=(a == PASSES - 1 and t % per == per - 1),
+                )
+
+        for a in range(PASSES - 1):
+            for c in range(len(H_WIDTHS)):
+                first_product(c, a)
+        gather_words(PASSES - 1, 0, S // 2)
+        gather_words(PASSES - 1, S // 2, S)
+        for c in range(len(H_WIDTHS)):
+            first_product(c, PASSES - 1)
+
+        h = [sb("h%d" % c, [P, PACK, w], F32) for c, w in enumerate(H_WIDTHS)]
+        h_bf = [sb("h_bf%d" % c, [P, w, PACK], BF16) for c, w in enumerate(H_WIDTHS)]
+        h_codes = [sb("h_codes%d" % c, [P, w], U32) for c, w in enumerate(H_WIDTHS)]
+        h_scales = [sb("h_scales%d" % c, [P, w], U8) for c, w in enumerate(H_WIDTHS)]
+
+        def h_out(c, ts):
+            for t in ts:
+                nc.scalar.activation(h[c][:, t, :], h_psum(c, t), ACT.Identity, bias=bq_t[:, t : t + 1])
+
+        def h_round(c):
+            dst = h_bf[c][:].rearrange("p (n i) t -> p n t i", i=PACK)
+            src = h[c][:].rearrange("p t (n i) -> p n t i", i=PACK)
+            if c < IL_ON_VECTOR:
+                nc.vector.tensor_copy(dst, src)
+            else:
+                nc.scalar.copy(dst, src)
+
+        def h_quantize(c):
+            nc.vector.quantize_mx(h_codes[c][:].bitcast(FP8X4), h_scales[c][:], h_bf[c][:].rearrange("p n t -> p (n t)"))
+
+        def chunk_of(s):
+            c = max(i for i in range(len(H_WIDTHS)) if starts[i] <= s * SUB)
+            o = s * SUB - starts[c]
+            return c, slice(o, o + SUB)
+
+        gate = {}
+        d_bf = [sb("d_bf%d" % s, [P, MB * SUB * PACK], BF16) for s in range(NSUB)]
+        d_codes = [sb("d_codes%d" % s, [P, MB * SUB], U32) for s in range(NSUB)]
+        d_scales = [sb("d_scales%d" % s, [P, MB * SUB], U8) for s in range(NSUB)]
+        res = [sb("res%d" % s, [P, PACK, SUB], F32) for s in range(NSUB)]
+        out_v = out.rearrange("(p t) j -> p t j", t=PACK)
+
+        def second_product(s, b):
+            c, cols = chunk_of(s)
+            e = bank(b, "e%d_%d" % (s, b))
+            for t in range(PACK):
+                m = slice(b * KP + t * P, b * KP + (t + 1) * P)
+                nc.tensor.matmul_mx(
+                    e[:, t * SUB : (t + 1) * SUB],
+                    lhsT=v2_codes[:, m].bitcast(FP8X4),
+                    lhsT_scale=v2_scales[:, m],
+                    rhs=h_codes[c][:, cols].bitcast(FP8X4),
+                    rhs_scale=h_scales[c][:, cols],
+                    start=True,
+                    stop=True,
+                )
+            gate[s, b] = keep.tile([P, SUB, PACK], F32, name="gate%d_%d" % (s, b), tag="gate", bufs=8, align_bytes=64)
+            nc.scalar.activation(gate[s, b][:], e[:].rearrange("p (t n) -> p n t", t=PACK), ACT.Sigmoid)
+
+        def weigh(s, b):
+            nc.vector.tensor_tensor(
+                d_bf[s][:, b * KP : (b + 1) * KP].rearrange("p (n t) -> p n t", t=PACK),
+                gate[s, b][:],
+                pw_t[:, b, :].unsqueeze(1).to_broadcast([P, SUB, PACK]),
+                ALU.mult,
+            )
+
+        def d_quantize(s):
+            nc.vector.quantize_mx(d_codes[s][:].bitcast(FP8X4), d_scales[s][:], d_bf[s][:])
+
+        x_banks = {}
+
+        def third_product(s):
+            x = bank(2 + s % 2, "x%d" % s)
+            x_banks[s] = x
+            for t in range(PACK):
+                for b in range(MB):
+                    n0 = b * H + t * P
+                    nc.tensor.matmul_mx(
+                        x[:, t * SUB : (t + 1) * SUB],
+                        lhsT=vm_codes[:, 2 * n0 : 2 * (n0 + P)].bitcast(FP4X4),
+                        lhsT_scale=vm_scale[:, n0 : n0 + P],
+                        rhs=d_codes[s][:, b * SUB : (b + 1) * SUB].bitcast(FP8X4),
+                        rhs_scale=d_scales[s][:, b * SUB : (b + 1) * SUB],
+                        start=(b == 0),
+                        stop=(b == MB - 1),
+                    )
+
+        def finish(s):
+            c, cols = chunk_of(s)
+            for t in range(PACK):
+                nc.vector.scalar_tensor_tensor(
+                    res[s][:, t, :], h[c][:, t, cols], rg_t[:, t : t + 1], x_banks[s][:, t * SUB : (t + 1) * SUB], ALU.mult, ALU.add
+                )
+            nc.sync.dma_start(out_v[:, :, s * SUB : (s + 1) * SUB], res[s][:])
+
+        h_out(0, range(PACK))
+        h_round(0)
+        h_out(1, range(PACK))
+        h_quantize(0)
+        h_round(1)
+        h_out(2, range(2))
+        h_quantize(1)
+        for s in range(NSUB + 2):
+            if s < NSUB:
+                second_product(s, 0)
+                weigh(s, 0)
+            if s == 1:
+                h_quantize(2)
+            if 1 <= s <= NSUB:
+                d_quantize(s - 1)
+                third_product(s - 1)
+            if s < NSUB:
+                second_product(s, 1)
+                weigh(s, 1)
+            if s >= 2:
+                finish(s - 2)
+            if s == 0:
+                h_out(2, range(2, 4))
+                h_round(2)
+            if s in (1, 3):
+                h_out((s + 5) // 2, range(PACK))
+            if s in (2, 4):
+                h_round((s + 4) // 2)
+            if s in (3, 5):
+                h_quantize((s + 3) // 2)

@@ -19,12 +19,20 @@ ALU = mybir.AluOpType
 P = 128
 PACK = 4
 KP = P * PACK
-PASSES = K // KP
-MB = S2 // KP
-SUB = 128
-NSUB = S // SUB
-H_WIDTHS = (128, 128, 256, 256, 256)
-IL_ON_VECTOR = 3
+K_PASSES = K // KP
+M_PASSES = S2 // KP
+QUADS = 4
+LIST_ROWS = 16
+SUB = P
+V_SCALE_ROW = 4
+
+WIDTHS = (128, 128, 256, 256, 128, 128)
+H_BANKS = ((0,), (1,), (2, 3), (4, 5), (6,), (7,))
+X_BANKS = ((2,), (3,), (4, 5), (2, 3), (4, 5), (6, 7))
+E_BANKS = (0, 1)
+EARLY_CHUNKS = 6
+ROUND_ON_VECTOR = 3
+GATE_BUFS = 6
 
 
 def tile_list_prior_art_expansion_kernel(
@@ -41,62 +49,65 @@ def tile_list_prior_art_expansion_kernel(
         def bank(k, name):
             return psum.tile([P, KP], F32, name=name, tag="bank%d" % k)
 
-        list1 = keep.tile([P, S // 16], U16, name="list1")
-        list2 = keep.tile([P, S2 // 16], U16, name="list2")
+        list1 = keep.tile([P, S // LIST_ROWS], U16, name="list1")
+        list2 = keep.tile([P, S2 // LIST_ROWS], U16, name="list2")
         t2_words = sb("t2_words", [P, T2], I32)
         t2_scales = sb("t2_scales", [P, T2], U8)
-        t_words = [sb("t_words%d" % a, [P, T], I32) for a in range(PASSES)]
+        t_words = [sb("t_words%d" % a, [P, T], I32) for a in range(K_PASSES)]
         t_scales = sb("t_scales", [P, T], U8)
-        w_raw = [sb("w_raw%d" % a, [P, PACK, H], F32) for a in range(PASSES)]
-        vm_raw = sb("vm_raw", [P, MB, H // 2], I32)
-        vm_raw_scales = sb("vm_raw_scales", [P, MB * H], U8)
+        w_raw = [sb("w_raw%d" % a, [P, PACK, H], F32) for a in range(K_PASSES)]
+        vm_raw = sb("vm_raw", [P, M_PASSES, H // 2], I32)
+        vm_raw_scales = sb("vm_raw_scales", [P, M_PASSES * H], U8)
         bq_t = sb("bq_t", [P, PACK], F32)
         rg_t = sb("rg_t", [P, PACK], F32)
-        pw_t = sb("pw_t", [P, MB, PACK], F32)
+        pw_t = sb("pw_t", [P, M_PASSES, PACK], F32)
         warm = sb("warm", [P, 2], F32)
 
-        nc.vector.memset(t2_scales[:].bitcast(I32), 0)
-        nc.gpsimd.memset(t_scales[:].bitcast(I32), 0)
-        nc.vector.memset(vm_raw_scales[:].bitcast(I32), 0)
-        nc.vector.memset(warm[:, 0:1], 0.0)
+        nc.gpsimd.memset(t2_scales[:].bitcast(I32), 0)
+        nc.vector.memset(t_scales[:].bitcast(I32), 0)
+        nc.gpsimd.memset(vm_raw_scales[:].bitcast(I32), 0)
+        nc.gpsimd.memset(warm[:, 0:1], 0.0)
         nc.scalar.activation(warm[:, 1:2], warm[:, 0:1], ACT.Sigmoid)
 
-        def words_of(src, a):
-            return src[a].rearrange("p n i -> p (n i)").bitcast(I32)
+        def load_words(dst, src, a):
+            nc.sync.dma_start(dst[:], src[a].rearrange("p n i -> p (n i)").bitcast(I32))
 
         def load_w(a):
             nc.sync.dma_start(w_raw[a][:], wq[a * KP : (a + 1) * KP, :].rearrange("(p i) r -> p i r", i=PACK))
 
         nc.sync.dma_start(list2[:], offs2)
-        nc.sync.dma_start(t2_words[:], words_of(tab2_words, 0))
-        for q in range(4):
-            nc.sync.dma_start(t2_scales[32 * q : 32 * q + 4, :].bitcast(I32), tab2_scales[0, 4 * q : 4 * q + 4, :].bitcast(I32))
+        load_words(t2_words, tab2_words, 0)
+        for r in range(PACK):
+            nc.sync.dma_start(t2_scales[r:P:32, :].bitcast(I32), tab2_scales[0, r:16:4, :].bitcast(I32))
         nc.sync.dma_start(list1[:], offs)
-        nc.sync.dma_start(t_words[0][:], words_of(tab_words, 0))
+        load_words(t_words[0], tab_words, 0)
         load_w(0)
-        nc.sync.dma_start(bq_t[:], bq.rearrange("(p t) -> p t", t=PACK))
-        nc.sync.dma_start(pw_t[:], pw.rearrange("(b p t) -> p b t", b=MB, t=PACK))
-        nc.sync.dma_start(rg_t[:], rg.rearrange("(p t) -> p t", t=PACK))
         nc.sync.dma_start(vm_raw[:], vm_words.rearrange("b p n -> p b n").bitcast(I32))
         load_w(1)
-        for q in range(4):
+        for r in range(PACK):
             nc.sync.dma_start(
-                vm_raw_scales[32 * q : 32 * q + 4, :].bitcast(I32).rearrange("r (b n) -> r b n", b=MB),
-                vm_scales[:, 4 * q : 4 * q + 4, :].rearrange("b r n -> r b n").bitcast(I32),
+                vm_raw_scales[r:P:32, :].bitcast(I32).rearrange("q (b n) -> q b n", b=M_PASSES),
+                vm_scales[:, r:16:4, :].rearrange("b q n -> q b n").bitcast(I32),
             )
         load_w(2)
-        for a in range(1, PASSES):
-            nc.sync.dma_start(t_words[a][:], words_of(tab_words, a))
-
-        for q in range(4):
+        load_words(t_words[1], tab_words, 1)
+        load_words(t_words[2], tab_words, 2)
+        nc.sync.dma_start(bq_t[:], bq.rearrange("(p t) -> p t", t=PACK))
+        nc.sync.dma_start(pw_t[:], pw.rearrange("(b p t) -> p b t", b=M_PASSES, t=PACK))
+        nc.sync.dma_start(rg_t[:], rg.rearrange("(p t) -> p t", t=PACK))
+        for q in range(QUADS):
+            first = 32 * q + V_SCALE_ROW
             nc.gpsimd.dma_start(
-                t_scales[32 * q : 32 * q + 4 * PASSES, :].bitcast(I32), tab_scales[:, 4 * q : 4 * q + 4, :].bitcast(I32)
+                t_scales[first : first + 4 * K_PASSES, :].bitcast(I32), tab_scales[:, 4 * q : 4 * q + 4, :].bitcast(I32)
             )
 
-        def deal(dst, src):
+        def deal(dst, src, walk):
             nc.vector.tensor_copy(
-                dst.rearrange("p (b t m) -> p b m t", b=MB, t=PACK), src.rearrange("p (b m t) -> p b m t", b=MB, t=PACK)
+                dst.rearrange("p (b t m) -> " + walk, b=M_PASSES, t=PACK),
+                src.rearrange("p (b m t) -> " + walk, b=M_PASSES, t=PACK),
             )
+
+        read_in_order, write_in_order = "p b m t", "p b t m"
 
         v2_picked = sb("v2_picked", [P, S2], U32)
         v2_picked_scales = sb("v2_picked_scales", [P, S2], U8)
@@ -104,189 +115,186 @@ def tile_list_prior_art_expansion_kernel(
         v2_scales = sb("v2_scales", [P, S2], U8)
         nc.vector.tensor_copy(v2_picked[:], t2_words[:].bitcast(U32).indirect(list2[:]))
         nc.vector.tensor_copy(v2_picked_scales[:], t2_scales[:].indirect(list2[:]))
-        deal(v2_codes[:], v2_picked[:])
-        deal(v2_scales[:], v2_picked_scales[:])
+        deal(v2_codes[:], v2_picked[:], read_in_order)
+        deal(v2_scales[:], v2_picked_scales[:], write_in_order)
 
-        v_codes = [sb("v_codes%d" % a, [P, S], U32) for a in range(PASSES)]
+        v_codes = [sb("v_codes%d" % a, [P, S], U32) for a in range(K_PASSES)]
         v_scales = sb("v_scales", [P, S], U8)
 
         def gather_words(a, j0, j1):
-            nc.vector.tensor_copy(v_codes[a][:, j0:j1], t_words[a][:].bitcast(U32).indirect(list1[:, j0 // 16 : j1 // 16]))
+            entries = list1[:, j0 // LIST_ROWS : j1 // LIST_ROWS]
+            nc.vector.tensor_copy(v_codes[a][:, j0:j1], t_words[a][:].bitcast(U32).indirect(entries))
 
-        w_codes = [sb("w_codes%d" % a, [P, H], U32) for a in range(PASSES)]
-        w_scales = [sb("w_scales%d" % a, [P, H], U8) for a in range(PASSES)]
-        w_bf = [sb("w_bf%d" % a, [P, H * PACK], BF16) for a in range(PASSES)]
-        for a in range(PASSES):
+        w_bf = [sb("w_bf%d" % a, [P, H * PACK], BF16) for a in range(K_PASSES)]
+        w_codes = [sb("w_codes%d" % a, [P, H], U32) for a in range(K_PASSES)]
+        w_scales = [sb("w_scales%d" % a, [P, H], U8) for a in range(K_PASSES)]
+        for a in range(K_PASSES):
             nc.scalar.copy(
-                w_bf[a][:].rearrange("p (t m i) -> p m i t", t=PACK, i=PACK),
-                w_raw[a][:].rearrange("p i (m t) -> p m i t", t=PACK),
+                w_bf[a][:].rearrange("p (t m i) -> p m t i", t=PACK, i=PACK),
+                w_raw[a][:].rearrange("p i (m t) -> p m t i", t=PACK),
             )
 
-        def quantize_w(a):
+        def w_quantize(a):
             nc.vector.quantize_mx(w_codes[a][:].bitcast(FP8X4), w_scales[a][:], w_bf[a][:])
 
-        vm_codes = sb("vm_codes", [P, MB * H * 2], U8)
-        vm_scale = sb("vm_scale", [P, MB * H], U8)
+        vm_codes = sb("vm_codes", [P, M_PASSES * H * 2], U8)
+        vm_dealt_scales = sb("vm_dealt_scales", [P, M_PASSES * H], U8)
 
         gather_words(0, 0, S)
         nc.vector.tensor_copy(v_scales[:], t_scales[:].indirect(list1[:]))
-        quantize_w(0)
-        deal(vm_codes[:].bitcast(U16), vm_raw[:].rearrange("p b n -> p (b n)").bitcast(U16))
-        quantize_w(1)
-        deal(vm_scale[:], vm_raw_scales[:])
-        quantize_w(2)
+        w_quantize(0)
+        deal(vm_codes[:].bitcast(U16), vm_raw[:].rearrange("p b n -> p (b n)").bitcast(U16), write_in_order)
+        w_quantize(1)
+        deal(vm_dealt_scales[:], vm_raw_scales[:], write_in_order)
+        w_quantize(2)
         gather_words(1, 0, S // 2)
         gather_words(1, S // 2, S)
 
-        starts = [sum(H_WIDTHS[:c]) for c in range(len(H_WIDTHS))]
-        h_banks = []
-        nb = 0
-        for c, w in enumerate(H_WIDTHS):
-            n = w // SUB
-            h_banks.append([bank(nb + u, "h_bank%d_%d" % (c, u)) for u in range(n)])
-            nb = nb + n
+        chunks = len(WIDTHS)
+        starts = [sum(WIDTHS[:c]) for c in range(chunks)]
 
-        def h_psum(c, t):
-            w = H_WIDTHS[c]
-            per = KP // w
-            return h_banks[c][t // per][:, (t % per) * w : (t % per + 1) * w]
+        def outputs_in(banks, width):
+            per_bank = PACK // len(banks)
+            return [banks[t // per_bank][:, (t % per_bank) * width : (t % per_bank + 1) * width] for t in range(PACK)]
+
+        h_psum = {}
 
         def first_product(c, a):
-            w = H_WIDTHS[c]
-            per = KP // w
-            cols = slice(starts[c], starts[c] + w)
+            per_bank = PACK // len(H_BANKS[c])
+            cols = slice(starts[c], starts[c] + WIDTHS[c])
+            if a == 0:
+                h_psum[c] = outputs_in([bank(k, "h%d_%d" % (c, k)) for k in H_BANKS[c]], WIDTHS[c])
             for t in range(PACK):
                 nc.tensor.matmul_mx(
-                    h_psum(c, t),
+                    h_psum[c][t],
                     lhsT=w_codes[a][:, t * P : (t + 1) * P].bitcast(FP8X4),
                     lhsT_scale=w_scales[a][:, t * P : (t + 1) * P],
                     rhs=v_codes[a][:, cols].bitcast(FP8X4),
-                    rhs_scale=v_scales[4 * a : P, cols],
-                    start=(a == 0 and t % per == 0),
-                    stop=(a == PASSES - 1 and t % per == per - 1),
+                    rhs_scale=v_scales[V_SCALE_ROW + 4 * a : P, cols],
+                    start=(a == 0 and t % per_bank == 0),
+                    stop=(a == K_PASSES - 1 and t % per_bank == per_bank - 1),
                 )
 
-        for a in range(PASSES - 1):
-            for c in range(len(H_WIDTHS)):
-                first_product(c, a)
-        gather_words(PASSES - 1, 0, S // 2)
-        gather_words(PASSES - 1, S // 2, S)
-        for c in range(len(H_WIDTHS)):
-            first_product(c, PASSES - 1)
+        h = [sb("h%d" % c, [P, PACK, w], F32) for c, w in enumerate(WIDTHS)]
+        h_bf = [sb("h_bf%d" % c, [P, w, PACK], BF16) for c, w in enumerate(WIDTHS)]
+        h_codes = [sb("h_codes%d" % c, [P, w], U32) for c, w in enumerate(WIDTHS)]
+        h_scales = [sb("h_scales%d" % c, [P, w], U8) for c, w in enumerate(WIDTHS)]
 
-        h = [sb("h%d" % c, [P, PACK, w], F32) for c, w in enumerate(H_WIDTHS)]
-        h_bf = [sb("h_bf%d" % c, [P, w, PACK], BF16) for c, w in enumerate(H_WIDTHS)]
-        h_codes = [sb("h_codes%d" % c, [P, w], U32) for c, w in enumerate(H_WIDTHS)]
-        h_scales = [sb("h_scales%d" % c, [P, w], U8) for c, w in enumerate(H_WIDTHS)]
-
-        def h_out(c, ts):
-            for t in ts:
-                nc.scalar.activation(h[c][:, t, :], h_psum(c, t), ACT.Identity, bias=bq_t[:, t : t + 1])
+        def h_out(c):
+            if c >= EARLY_CHUNKS:
+                for a in range(K_PASSES):
+                    first_product(c, a)
+            for t in range(PACK):
+                nc.scalar.activation(h[c][:, t, :], h_psum[c][t], ACT.Identity, bias=bq_t[:, t : t + 1])
 
         def h_round(c):
-            dst = h_bf[c][:].rearrange("p (n i) t -> p n t i", i=PACK)
-            src = h[c][:].rearrange("p t (n i) -> p n t i", i=PACK)
-            if c < IL_ON_VECTOR:
-                nc.vector.tensor_copy(dst, src)
-            else:
-                nc.scalar.copy(dst, src)
+            copy = nc.vector.tensor_copy if c < ROUND_ON_VECTOR else nc.scalar.copy
+            copy(h_bf[c][:].rearrange("p (n i) t -> p n t i", i=PACK), h[c][:].rearrange("p t (n i) -> p n t i", i=PACK))
 
         def h_quantize(c):
             nc.vector.quantize_mx(h_codes[c][:].bitcast(FP8X4), h_scales[c][:], h_bf[c][:].rearrange("p n t -> p (n t)"))
 
-        def chunk_of(s):
-            c = max(i for i in range(len(H_WIDTHS)) if starts[i] <= s * SUB)
-            o = s * SUB - starts[c]
-            return c, slice(o, o + SUB)
-
         gate = {}
-        d_bf = [sb("d_bf%d" % s, [P, MB * SUB * PACK], BF16) for s in range(NSUB)]
-        d_codes = [sb("d_codes%d" % s, [P, MB * SUB], U32) for s in range(NSUB)]
-        d_scales = [sb("d_scales%d" % s, [P, MB * SUB], U8) for s in range(NSUB)]
-        res = [sb("res%d" % s, [P, PACK, SUB], F32) for s in range(NSUB)]
-        out_v = out.rearrange("(p t) j -> p t j", t=PACK)
+        d_bf = [sb("d_bf%d" % c, [P, M_PASSES * w * PACK], BF16) for c, w in enumerate(WIDTHS)]
+        d_codes = [sb("d_codes%d" % c, [P, M_PASSES * w], U32) for c, w in enumerate(WIDTHS)]
+        d_scales = [sb("d_scales%d" % c, [P, M_PASSES * w], U8) for c, w in enumerate(WIDTHS)]
 
-        def second_product(s, b):
-            c, cols = chunk_of(s)
-            e = bank(b, "e%d_%d" % (s, b))
-            for t in range(PACK):
-                m = slice(b * KP + t * P, b * KP + (t + 1) * P)
-                nc.tensor.matmul_mx(
-                    e[:, t * SUB : (t + 1) * SUB],
-                    lhsT=v2_codes[:, m].bitcast(FP8X4),
-                    lhsT_scale=v2_scales[:, m],
-                    rhs=h_codes[c][:, cols].bitcast(FP8X4),
-                    rhs_scale=h_scales[c][:, cols],
-                    start=True,
-                    stop=True,
+        def second_product(c, b):
+            gate[c, b] = keep.tile(
+                [P, WIDTHS[c] * PACK], F32, name="gate%d_%d" % (c, b), tag="gate", bufs=GATE_BUFS, align_bytes=64
+            )
+            for u in range(WIDTHS[c] // SUB):
+                cols = slice(u * SUB, (u + 1) * SUB)
+                turn = (M_PASSES * starts[c] + b * WIDTHS[c]) // SUB + u
+                e = bank(E_BANKS[turn % len(E_BANKS)], "e%d" % turn)
+                for t in range(PACK):
+                    m = slice(b * KP + t * P, b * KP + (t + 1) * P)
+                    nc.tensor.matmul_mx(
+                        e[:, t * SUB : (t + 1) * SUB],
+                        lhsT=v2_codes[:, m].bitcast(FP8X4),
+                        lhsT_scale=v2_scales[:, m],
+                        rhs=h_codes[c][:, cols].bitcast(FP8X4),
+                        rhs_scale=h_scales[c][:, cols],
+                        start=True,
+                        stop=True,
+                    )
+                nc.scalar.activation(
+                    gate[c, b][:, u * KP : (u + 1) * KP].rearrange("p (n t) -> p n t", t=PACK),
+                    e[:].rearrange("p (t n) -> p n t", t=PACK),
+                    ACT.Sigmoid,
                 )
-            gate[s, b] = keep.tile([P, SUB, PACK], F32, name="gate%d_%d" % (s, b), tag="gate", bufs=8, align_bytes=64)
-            nc.scalar.activation(gate[s, b][:], e[:].rearrange("p (t n) -> p n t", t=PACK), ACT.Sigmoid)
 
-        def weigh(s, b):
+        def weigh(c, b):
+            w = WIDTHS[c]
             nc.vector.tensor_tensor(
-                d_bf[s][:, b * KP : (b + 1) * KP].rearrange("p (n t) -> p n t", t=PACK),
-                gate[s, b][:],
-                pw_t[:, b, :].unsqueeze(1).to_broadcast([P, SUB, PACK]),
+                d_bf[c][:, b * w * PACK : (b + 1) * w * PACK].rearrange("p (n t) -> p n t", t=PACK),
+                gate[c, b][:].rearrange("p (n t) -> p n t", t=PACK),
+                pw_t[:, b, :].unsqueeze(1).to_broadcast([P, w, PACK]),
                 ALU.mult,
             )
 
-        def d_quantize(s):
-            nc.vector.quantize_mx(d_codes[s][:].bitcast(FP8X4), d_scales[s][:], d_bf[s][:])
+        x_psum = {}
 
-        x_banks = {}
-
-        def third_product(s):
-            x = bank(2 + s % 2, "x%d" % s)
-            x_banks[s] = x
+        def third_product(c):
+            w = WIDTHS[c]
+            nc.vector.quantize_mx(d_codes[c][:].bitcast(FP8X4), d_scales[c][:], d_bf[c][:])
+            x_psum[c] = outputs_in([bank(k, "x%d_%d" % (c, k)) for k in X_BANKS[c]], w)
             for t in range(PACK):
-                for b in range(MB):
-                    n0 = b * H + t * P
-                    nc.tensor.matmul_mx(
-                        x[:, t * SUB : (t + 1) * SUB],
-                        lhsT=vm_codes[:, 2 * n0 : 2 * (n0 + P)].bitcast(FP4X4),
-                        lhsT_scale=vm_scale[:, n0 : n0 + P],
-                        rhs=d_codes[s][:, b * SUB : (b + 1) * SUB].bitcast(FP8X4),
-                        rhs_scale=d_scales[s][:, b * SUB : (b + 1) * SUB],
-                        start=(b == 0),
-                        stop=(b == MB - 1),
-                    )
+                for u in range(w // SUB):
+                    for b in range(M_PASSES):
+                        n0 = b * H + t * P
+                        cols = slice(b * w + u * SUB, b * w + (u + 1) * SUB)
+                        nc.tensor.matmul_mx(
+                            x_psum[c][t][:, u * SUB : (u + 1) * SUB],
+                            lhsT=vm_codes[:, 2 * n0 : 2 * (n0 + P)].bitcast(FP4X4),
+                            lhsT_scale=vm_dealt_scales[:, n0 : n0 + P],
+                            rhs=d_codes[c][:, cols].bitcast(FP8X4),
+                            rhs_scale=d_scales[c][:, cols],
+                            start=(b == 0),
+                            stop=(b == M_PASSES - 1),
+                        )
 
-        def finish(s):
-            c, cols = chunk_of(s)
-            for t in range(PACK):
-                nc.vector.scalar_tensor_tensor(
-                    res[s][:, t, :], h[c][:, t, cols], rg_t[:, t : t + 1], x_banks[s][:, t * SUB : (t + 1) * SUB], ALU.mult, ALU.add
-                )
-            nc.sync.dma_start(out_v[:, :, s * SUB : (s + 1) * SUB], res[s][:])
+        res = [sb("res%d" % c, [P, PACK, w], F32) for c, w in enumerate(WIDTHS)]
+        out_rows = out.rearrange("(p t) j -> p t j", t=PACK)
 
-        h_out(0, range(PACK))
-        h_round(0)
-        h_out(1, range(PACK))
-        h_quantize(0)
-        h_round(1)
-        h_out(2, range(2))
-        h_quantize(1)
-        for s in range(NSUB + 2):
-            if s < NSUB:
-                second_product(s, 0)
-                weigh(s, 0)
-            if s == 1:
-                h_quantize(2)
-            if 1 <= s <= NSUB:
-                d_quantize(s - 1)
-                third_product(s - 1)
-            if s < NSUB:
-                second_product(s, 1)
-                weigh(s, 1)
-            if s >= 2:
-                finish(s - 2)
-            if s == 0:
-                h_out(2, range(2, 4))
-                h_round(2)
-            if s in (1, 3):
-                h_out((s + 5) // 2, range(PACK))
-            if s in (2, 4):
-                h_round((s + 4) // 2)
-            if s in (3, 5):
-                h_quantize((s + 3) // 2)
+        def finish(c, half):
+            ts = slice(2 * half, 2 * half + 2)
+            for t in range(ts.start, ts.stop):
+                nc.vector.scalar_tensor_tensor(res[c][:, t, :], h[c][:, t, :], rg_t[:, t : t + 1], x_psum[c][t], ALU.mult, ALU.add)
+            nc.sync.dma_start(out_rows[:, ts, starts[c] : starts[c] + WIDTHS[c]], res[c][:, ts, :])
+
+        for a in range(K_PASSES - 1):
+            for c in range(EARLY_CHUNKS):
+                first_product(c, a)
+        gather_words(K_PASSES - 1, 0, S // 2)
+        gather_words(K_PASSES - 1, S // 2, S)
+        for c in range(EARLY_CHUNKS):
+            first_product(c, K_PASSES - 1)
+
+        for c in range(2):
+            h_out(c)
+            h_round(c)
+        for c in range(2):
+            h_quantize(c)
+        for b in range(M_PASSES):
+            second_product(0, b)
+        for c in range(chunks):
+            if c + 2 < chunks:
+                h_out(c + 2)
+            if c + 1 < chunks:
+                second_product(c + 1, 0)
+            if c + 2 < chunks:
+                h_round(c + 2)
+            if c + 1 < chunks:
+                second_product(c + 1, 1)
+            weigh(c, 0)
+            weigh(c, 1)
+            if c + 2 < chunks:
+                h_quantize(c + 2)
+            if c > 0:
+                finish(c - 1, 0)
+            third_product(c)
+            if c > 0:
+                finish(c - 1, 1)
+        finish(chunks - 1, 0)
+        finish(chunks - 1, 1)

@@ -28,11 +28,11 @@ V_SCALE_ROW = 4
 
 WIDTHS = (128, 128, 256, 256, 128, 128)
 H_BANKS = ((0,), (1,), (2, 3), (4, 5), (6,), (7,))
-X_BANKS = ((2,), (3,), (4, 5), (2, 3), (4, 5), (6, 7))
-E_BANKS = (0, 1)
-EARLY_CHUNKS = 6
-ROUND_ON_VECTOR = 3
-GATE_BUFS = 6
+X_BANKS = ((3,), (4,), (5, 6), (7, 3), (4, 5), (6, 7))
+E_BANKS = (0, 1, 2)
+ROUND_ON_VECTOR = (1, 2, 3)
+WEIGH_ON_SCALAR = ((4, 0), (5, 0))
+GATE_BUFS = 8
 
 
 def tile_list_prior_art_expansion_kernel(
@@ -75,24 +75,24 @@ def tile_list_prior_art_expansion_kernel(
         def load_w(a):
             nc.sync.dma_start(w_raw[a][:], wq[a * KP : (a + 1) * KP, :].rearrange("(p i) r -> p i r", i=PACK))
 
-        nc.sync.dma_start(list2[:], offs2)
-        load_words(t2_words, tab2_words, 0)
-        for r in range(PACK):
-            nc.sync.dma_start(t2_scales[r:P:32, :].bitcast(I32), tab2_scales[0, r:16:4, :].bitcast(I32))
         nc.sync.dma_start(list1[:], offs)
         load_words(t_words[0], tab_words, 0)
         load_w(0)
-        nc.sync.dma_start(vm_raw[:], vm_words.rearrange("b p n -> p b n").bitcast(I32))
+        nc.sync.dma_start(bq_t[:], bq.rearrange("(p t) -> p t", t=PACK))
+        nc.sync.dma_start(list2[:], offs2)
+        for r in range(PACK):
+            nc.sync.dma_start(t2_scales[r:P:32, :].bitcast(I32), tab2_scales[0, r:16:4, :].bitcast(I32))
         load_w(1)
+        load_words(t_words[1], tab_words, 1)
+        nc.sync.dma_start(vm_raw[:], vm_words.rearrange("b p n -> p b n").bitcast(I32))
         for r in range(PACK):
             nc.sync.dma_start(
                 vm_raw_scales[r:P:32, :].bitcast(I32).rearrange("q (b n) -> q b n", b=M_PASSES),
                 vm_scales[:, r:16:4, :].rearrange("b q n -> q b n").bitcast(I32),
             )
         load_w(2)
-        load_words(t_words[1], tab_words, 1)
         load_words(t_words[2], tab_words, 2)
-        nc.sync.dma_start(bq_t[:], bq.rearrange("(p t) -> p t", t=PACK))
+        load_words(t2_words, tab2_words, 0)
         nc.sync.dma_start(pw_t[:], pw.rearrange("(b p t) -> p b t", b=M_PASSES, t=PACK))
         nc.sync.dma_start(rg_t[:], rg.rearrange("(p t) -> p t", t=PACK))
         for q in range(QUADS):
@@ -103,20 +103,21 @@ def tile_list_prior_art_expansion_kernel(
 
         def deal(dst, src, walk):
             nc.vector.tensor_copy(
-                dst.rearrange("p (b t m) -> " + walk, b=M_PASSES, t=PACK),
-                src.rearrange("p (b m t) -> " + walk, b=M_PASSES, t=PACK),
+                dst.rearrange("p (b t m) -> " + walk, m=P, t=PACK),
+                src.rearrange("p (b m t) -> " + walk, m=P, t=PACK),
             )
 
         read_in_order, write_in_order = "p b m t", "p b t m"
 
-        v2_picked = sb("v2_picked", [P, S2], U32)
         v2_picked_scales = sb("v2_picked_scales", [P, S2], U8)
-        v2_codes = sb("v2_codes", [P, S2], U32)
+        v2_codes = [sb("v2_codes%d" % b, [P, KP], U32) for b in range(M_PASSES)]
         v2_scales = sb("v2_scales", [P, S2], U8)
-        nc.vector.tensor_copy(v2_picked[:], t2_words[:].bitcast(U32).indirect(list2[:]))
-        nc.vector.tensor_copy(v2_picked_scales[:], t2_scales[:].indirect(list2[:]))
-        deal(v2_codes[:], v2_picked[:], read_in_order)
-        deal(v2_scales[:], v2_picked_scales[:], write_in_order)
+
+        def gather_patents(b):
+            entries = list2[:, b * KP // LIST_ROWS : (b + 1) * KP // LIST_ROWS]
+            picked = keep.tile([P, KP], U32, name="picked%d" % b, tag="picked", align_bytes=64)
+            nc.vector.tensor_copy(picked[:], t2_words[:].bitcast(U32).indirect(entries))
+            deal(v2_codes[b][:], picked[:], read_in_order)
 
         v_codes = [sb("v_codes%d" % a, [P, S], U32) for a in range(K_PASSES)]
         v_scales = sb("v_scales", [P, S], U8)
@@ -143,16 +144,16 @@ def tile_list_prior_art_expansion_kernel(
         gather_words(0, 0, S)
         nc.vector.tensor_copy(v_scales[:], t_scales[:].indirect(list1[:]))
         w_quantize(0)
-        deal(vm_codes[:].bitcast(U16), vm_raw[:].rearrange("p b n -> p (b n)").bitcast(U16), write_in_order)
+        nc.vector.tensor_copy(v2_picked_scales[:], t2_scales[:].indirect(list2[:]))
         w_quantize(1)
+        deal(v2_scales[:], v2_picked_scales[:], write_in_order)
+        gather_words(1, 0, S)
+        deal(vm_codes[:].bitcast(U16), vm_raw[:].rearrange("p b n -> p (b n)").bitcast(U16), write_in_order)
         deal(vm_dealt_scales[:], vm_raw_scales[:], write_in_order)
         w_quantize(2)
-        gather_words(1, 0, S // 2)
-        gather_words(1, S // 2, S)
 
         chunks = len(WIDTHS)
         starts = [sum(WIDTHS[:c]) for c in range(chunks)]
-
         def outputs_in(banks, width):
             per_bank = PACK // len(banks)
             return [banks[t // per_bank][:, (t % per_bank) * width : (t % per_bank + 1) * width] for t in range(PACK)]
@@ -180,16 +181,16 @@ def tile_list_prior_art_expansion_kernel(
         h_codes = [sb("h_codes%d" % c, [P, w], U32) for c, w in enumerate(WIDTHS)]
         h_scales = [sb("h_scales%d" % c, [P, w], U8) for c, w in enumerate(WIDTHS)]
 
+        def h_of(c):
+            return h[c][:]
+
         def h_out(c):
-            if c >= EARLY_CHUNKS:
-                for a in range(K_PASSES):
-                    first_product(c, a)
             for t in range(PACK):
                 nc.scalar.activation(h[c][:, t, :], h_psum[c][t], ACT.Identity, bias=bq_t[:, t : t + 1])
 
         def h_round(c):
-            copy = nc.vector.tensor_copy if c < ROUND_ON_VECTOR else nc.scalar.copy
-            copy(h_bf[c][:].rearrange("p (n i) t -> p n t i", i=PACK), h[c][:].rearrange("p t (n i) -> p n t i", i=PACK))
+            copy = nc.vector.tensor_copy if c in ROUND_ON_VECTOR else nc.scalar.copy
+            copy(h_bf[c][:].rearrange("p (n i) t -> p n t i", i=PACK), h_of(c).rearrange("p t (n i) -> p n t i", i=PACK))
 
         def h_quantize(c):
             nc.vector.quantize_mx(h_codes[c][:].bitcast(FP8X4), h_scales[c][:], h_bf[c][:].rearrange("p n t -> p (n t)"))
@@ -211,21 +212,36 @@ def tile_list_prior_art_expansion_kernel(
                     m = slice(b * KP + t * P, b * KP + (t + 1) * P)
                     nc.tensor.matmul_mx(
                         e[:, t * SUB : (t + 1) * SUB],
-                        lhsT=v2_codes[:, m].bitcast(FP8X4),
+                        lhsT=v2_codes[b][:, t * P : (t + 1) * P].bitcast(FP8X4),
                         lhsT_scale=v2_scales[:, m],
                         rhs=h_codes[c][:, cols].bitcast(FP8X4),
                         rhs_scale=h_scales[c][:, cols],
                         start=True,
                         stop=True,
                     )
-                nc.scalar.activation(
-                    gate[c, b][:, u * KP : (u + 1) * KP].rearrange("p (n t) -> p n t", t=PACK),
-                    e[:].rearrange("p (t n) -> p n t", t=PACK),
-                    ACT.Sigmoid,
-                )
+                if (c, b) in WEIGH_ON_SCALAR:
+                    nc.scalar.activation(gate[c, b][:, u * KP : (u + 1) * KP], e[:], ACT.Sigmoid)
+                else:
+                    nc.scalar.activation(
+                        gate[c, b][:, u * KP : (u + 1) * KP].rearrange("p (n t) -> p n t", t=PACK),
+                        e[:].rearrange("p (t n) -> p n t", t=PACK),
+                        ACT.Sigmoid,
+                    )
 
         def weigh(c, b):
             w = WIDTHS[c]
+            if (c, b) in WEIGH_ON_SCALAR:
+                rows = sb("d_rows%d_%d" % (c, b), [P, PACK, w], BF16)
+                by_t = gate[c, b][:].rearrange("p (u t n) -> p t u n", t=PACK, n=SUB)
+                for t in range(PACK):
+                    nc.scalar.activation(
+                        rows[:, t, :].rearrange("p (u n) -> p u n", n=SUB), by_t[:, t], ACT.Copy, scale=pw_t[:, b, t : t + 1]
+                    )
+                nc.scalar.copy(
+                    d_bf[c][:, b * w * PACK : (b + 1) * w * PACK].rearrange("p (n i t) -> p n t i", i=PACK, t=PACK),
+                    rows[:].rearrange("p t (n i) -> p n t i", i=PACK),
+                )
+                return
             nc.vector.tensor_tensor(
                 d_bf[c][:, b * w * PACK : (b + 1) * w * PACK].rearrange("p (n t) -> p n t", t=PACK),
                 gate[c, b][:].rearrange("p (n t) -> p n t", t=PACK),
@@ -235,66 +251,82 @@ def tile_list_prior_art_expansion_kernel(
 
         x_psum = {}
 
-        def third_product(c):
+        def d_quantize(c, b0, b1):
             w = WIDTHS[c]
-            nc.vector.quantize_mx(d_codes[c][:].bitcast(FP8X4), d_scales[c][:], d_bf[c][:])
-            x_psum[c] = outputs_in([bank(k, "x%d_%d" % (c, k)) for k in X_BANKS[c]], w)
-            for t in range(PACK):
-                for u in range(w // SUB):
-                    for b in range(M_PASSES):
-                        n0 = b * H + t * P
-                        cols = slice(b * w + u * SUB, b * w + (u + 1) * SUB)
-                        nc.tensor.matmul_mx(
-                            x_psum[c][t][:, u * SUB : (u + 1) * SUB],
-                            lhsT=vm_codes[:, 2 * n0 : 2 * (n0 + P)].bitcast(FP4X4),
-                            lhsT_scale=vm_dealt_scales[:, n0 : n0 + P],
-                            rhs=d_codes[c][:, cols].bitcast(FP8X4),
-                            rhs_scale=d_scales[c][:, cols],
-                            start=(b == 0),
-                            stop=(b == M_PASSES - 1),
-                        )
+            cols = slice(b0 * w, b1 * w)
+            nc.vector.quantize_mx(
+                d_codes[c][:, cols].bitcast(FP8X4), d_scales[c][:, cols], d_bf[c][:, b0 * w * PACK : b1 * w * PACK]
+            )
 
-        res = [sb("res%d" % c, [P, PACK, w], F32) for c, w in enumerate(WIDTHS)]
+        def third_product(c, b):
+            w = WIDTHS[c]
+            per_bank = PACK // len(X_BANKS[c])
+            if b == 0:
+                banks = [bank(k, "x%d_%d" % (c, k)) for k in X_BANKS[c]]
+                x_psum[c] = [banks[t // per_bank][:, (t % per_bank) * w : (t % per_bank + 1) * w] for t in range(PACK)]
+            for t in range(PACK):
+                n0 = b * H + t * P
+                for u in range(w // SUB):
+                    cols = slice(b * w + u * SUB, b * w + (u + 1) * SUB)
+                    nc.tensor.matmul_mx(
+                        x_psum[c][t][:, u * SUB : (u + 1) * SUB],
+                        lhsT=vm_codes[:, 2 * n0 : 2 * (n0 + P)].bitcast(FP4X4),
+                        lhsT_scale=vm_dealt_scales[:, n0 : n0 + P],
+                        rhs=d_codes[c][:, cols].bitcast(FP8X4),
+                        rhs_scale=d_scales[c][:, cols],
+                        start=(b == 0 and t % per_bank == 0 and u == 0),
+                        stop=(b == M_PASSES - 1 and t % per_bank == per_bank - 1 and u == w // SUB - 1),
+                    )
+
         out_rows = out.rearrange("(p t) j -> p t j", t=PACK)
 
         def finish(c, half):
             ts = slice(2 * half, 2 * half + 2)
             for t in range(ts.start, ts.stop):
-                nc.vector.scalar_tensor_tensor(res[c][:, t, :], h[c][:, t, :], rg_t[:, t : t + 1], x_psum[c][t], ALU.mult, ALU.add)
-            nc.sync.dma_start(out_rows[:, ts, starts[c] : starts[c] + WIDTHS[c]], res[c][:, ts, :])
+                nc.vector.scalar_tensor_tensor(h[c][:, t, :], h[c][:, t, :], rg_t[:, t : t + 1], x_psum[c][t], ALU.mult, ALU.add)
+            nc.sync.dma_start(out_rows[:, ts, starts[c] : starts[c] + WIDTHS[c]], h[c][:, ts, :])
 
         for a in range(K_PASSES - 1):
-            for c in range(EARLY_CHUNKS):
+            for c in range(chunks):
                 first_product(c, a)
         gather_words(K_PASSES - 1, 0, S // 2)
         gather_words(K_PASSES - 1, S // 2, S)
-        for c in range(EARLY_CHUNKS):
-            first_product(c, K_PASSES - 1)
-
-        for c in range(2):
-            h_out(c)
-            h_round(c)
-        for c in range(2):
-            h_quantize(c)
-        for b in range(M_PASSES):
-            second_product(0, b)
         for c in range(chunks):
-            if c + 2 < chunks:
+            first_product(c, K_PASSES - 1)
+        for b in range(M_PASSES):
+            h_out(b)
+            gather_patents(b)
+            h_round(b)
+            h_quantize(b)
+            second_product(0, b)
+        last = chunks - 1
+        for c in range(chunks):
+            if c + 2 <= last:
                 h_out(c + 2)
-            if c + 1 < chunks:
+            if c + 1 <= last:
                 second_product(c + 1, 0)
-            if c + 2 < chunks:
+            if c + 2 <= last:
                 h_round(c + 2)
-            if c + 1 < chunks:
+            if c + 1 <= last:
                 second_product(c + 1, 1)
             weigh(c, 0)
-            weigh(c, 1)
-            if c + 2 < chunks:
+            if c + 2 <= last:
                 h_quantize(c + 2)
-            if c > 0:
+            if c == last:
                 finish(c - 1, 0)
-            third_product(c)
-            if c > 0:
+                d_quantize(c, 0, 1)
+                third_product(c, 0)
+            weigh(c, 1)
+            if 0 < c < last:
+                finish(c - 1, 0)
+            if c == last:
                 finish(c - 1, 1)
-        finish(chunks - 1, 0)
-        finish(chunks - 1, 1)
+                d_quantize(c, 1, 2)
+            else:
+                d_quantize(c, 0, M_PASSES)
+                third_product(c, 0)
+            third_product(c, 1)
+            if 0 < c < last:
+                finish(c - 1, 1)
+        finish(last, 0)
+        finish(last, 1)

@@ -107,17 +107,17 @@ def tile_list_prior_art_expansion_kernel(
                 src.rearrange("p (b m t) -> " + walk, m=P, t=PACK),
             )
 
-        read_in_order, write_in_order = "p b m t", "p b t m"
+        write_in_order = "p b t m"
 
         v2_picked_scales = sb("v2_picked_scales", [P, S2], U8)
-        v2_codes = [sb("v2_codes%d" % b, [P, KP], U32) for b in range(M_PASSES)]
+        v2_codes = {}
         v2_scales = sb("v2_scales", [P, S2], U8)
 
         def gather_patents(b):
             entries = list2[:, b * KP // LIST_ROWS : (b + 1) * KP // LIST_ROWS]
-            picked = keep.tile([P, KP], U32, name="picked%d" % b, tag="picked", align_bytes=64)
-            nc.vector.tensor_copy(picked[:], t2_words[:].bitcast(U32).indirect(entries))
-            deal(v2_codes[b][:], picked[:], read_in_order)
+            v2_codes[b] = keep.tile([P, KP], U32, name="v2_codes%d" % b, tag="h_bf0" if b else "v2_first", align_bytes=64)
+            dealt = v2_codes[b][:].rearrange("p (t m) -> p m t", t=PACK)
+            nc.vector.tensor_copy(dealt, t2_words[:].bitcast(U32).indirect(entries))
 
         v_codes = [sb("v_codes%d" % a, [P, S], U32) for a in range(K_PASSES)]
         v_scales = sb("v_scales", [P, S], U8)
@@ -293,16 +293,22 @@ def tile_list_prior_art_expansion_kernel(
         gather_words(K_PASSES - 1, S // 2, S)
         for c in range(chunks):
             first_product(c, K_PASSES - 1)
-        for b in range(M_PASSES):
-            h_out(b)
-            gather_patents(b)
-            h_round(b)
-            h_quantize(b)
-            second_product(0, b)
+        h_out(0)
+        gather_patents(0)
+        h_round(0)
+        h_quantize(0)
+        h_out(1)
+        gather_patents(1)
+        second_product(0, 0)
+        h_round(1)
+        h_quantize(1)
+        for c in range(2, 4):
+            h_out(c)
+        second_product(0, 1)
         last = chunks - 1
         for c in range(chunks):
-            if c + 2 <= last:
-                h_out(c + 2)
+            if c + 4 <= last:
+                h_out(c + 4)
             if c + 1 <= last:
                 second_product(c + 1, 0)
             if c + 2 <= last:

@@ -83,14 +83,14 @@ def tile_list_prior_art_expansion_kernel(
         for r in range(PACK):
             nc.sync.dma_start(t2_scales[r:P:32, :].bitcast(I32), tab2_scales[0, r:16:4, :].bitcast(I32))
         load_w(1)
-        load_words(t_words[1], tab_words, 1)
         nc.sync.dma_start(vm_raw[:], vm_words.rearrange("b p n -> p b n").bitcast(I32))
+        load_w(2)
         for r in range(PACK):
             nc.sync.dma_start(
                 vm_raw_scales[r:P:32, :].bitcast(I32).rearrange("q (b n) -> q b n", b=M_PASSES),
                 vm_scales[:, r:16:4, :].rearrange("b q n -> q b n").bitcast(I32),
             )
-        load_w(2)
+        load_words(t_words[1], tab_words, 1)
         load_words(t_words[2], tab_words, 2)
         load_words(t2_words, tab2_words, 0)
         nc.sync.dma_start(pw_t[:], pw.rearrange("(b p t) -> p b t", b=M_PASSES, t=PACK))
@@ -147,10 +147,11 @@ def tile_list_prior_art_expansion_kernel(
         nc.vector.tensor_copy(v2_picked_scales[:], t2_scales[:].indirect(list2[:]))
         w_quantize(1)
         deal(v2_scales[:], v2_picked_scales[:], write_in_order)
-        gather_words(1, 0, S)
         deal(vm_codes[:].bitcast(U16), vm_raw[:].rearrange("p b n -> p (b n)").bitcast(U16), write_in_order)
         deal(vm_dealt_scales[:], vm_raw_scales[:], write_in_order)
         w_quantize(2)
+        gather_words(1, 0, S // 2)
+        gather_words(1, S // 2, S)
 
         chunks = len(WIDTHS)
         starts = [sum(WIDTHS[:c]) for c in range(chunks)]

@@ -1,6 +1,7 @@
 from contextlib import ExitStack
 
 import concourse.mybir as mybir
+from concourse.masks import make_identity
 
 K, H, T, S, T2, S2 = 1536, 512, 4096, 1024, 2048, 1024
 FLOPS = 2 * S * (K * H + H * S2 + S2 * H)
@@ -26,13 +27,16 @@ LIST_ROWS = 16
 SUB = P
 V_SCALE_ROW = 4
 
-WIDTHS = (128, 128, 256, 256, 128, 128)
-H_BANKS = ((0,), (1,), (2, 3), (4, 5), (6,), (7,))
-X_BANKS = ((3,), (4,), (5, 6), (7, 3), (4, 5), (6, 7))
-E_BANKS = (0, 1, 2)
-ROUND_ON_VECTOR = (1, 2, 3)
-WEIGH_ON_SCALAR = ((4, 0), (5, 0))
-GATE_BUFS = 8
+H_WIDTH = 256
+H_BANKS = ((0, 1), (2, 3), (4, 5), (6, 0))
+E_BANKS = (1, 2, 3)
+PW_BANK = 7
+WIDTHS = (256, 256, 256, 128, 128)
+X_BANKS = ((4, 5), (6, 0), (4, 5), (6, 0), (4, 5))
+GPSIMD_CLAIMS = (128, 192, 192, 128, 0)
+WEIGH_ON_SCALAR = ((3, 1), (4, 1))
+AHEAD = 2
+OVERLAP = 32
 
 
 def tile_list_prior_art_expansion_kernel(
@@ -60,12 +64,15 @@ def tile_list_prior_art_expansion_kernel(
         vm_raw_scales = sb("vm_raw_scales", [P, M_PASSES * H], U8)
         bq_t = sb("bq_t", [P, PACK], F32)
         rg_t = sb("rg_t", [P, PACK], F32)
-        pw_t = sb("pw_t", [P, M_PASSES, PACK], F32)
+        pw_pad = sb("pw_pad", [P, P], F32)
+        pw_t = pw_pad[:, 0 : M_PASSES * PACK].rearrange("p (b t) -> p b t", t=PACK)
+        ident = sb("ident", [P, P], F32)
         warm = sb("warm", [P, 2], F32)
 
         nc.gpsimd.memset(t2_scales[:].bitcast(I32), 0)
         nc.vector.memset(t_scales[:].bitcast(I32), 0)
         nc.gpsimd.memset(vm_raw_scales[:].bitcast(I32), 0)
+        nc.gpsimd.memset(pw_pad[:], 0.0)
         nc.gpsimd.memset(warm[:, 0:1], 0.0)
         nc.scalar.activation(warm[:, 1:2], warm[:, 0:1], ACT.Sigmoid)
 
@@ -90,16 +97,24 @@ def tile_list_prior_art_expansion_kernel(
                 vm_raw_scales[r:P:32, :].bitcast(I32).rearrange("q (b n) -> q b n", b=M_PASSES),
                 vm_scales[:, r:16:4, :].rearrange("b q n -> q b n").bitcast(I32),
             )
+        nc.sync.dma_start(pw_t, pw.rearrange("(b p t) -> p b t", b=M_PASSES, t=PACK))
         load_words(t_words[1], tab_words, 1)
         load_words(t_words[2], tab_words, 2)
         load_words(t2_words, tab2_words, 0)
-        nc.sync.dma_start(pw_t[:], pw.rearrange("(b p t) -> p b t", b=M_PASSES, t=PACK))
         nc.sync.dma_start(rg_t[:], rg.rearrange("(p t) -> p t", t=PACK))
         for q in range(QUADS):
             first = 32 * q + V_SCALE_ROW
             nc.gpsimd.dma_start(
                 t_scales[first : first + 4 * K_PASSES, :].bitcast(I32), tab_scales[:, 4 * q : 4 * q + 4, :].bitcast(I32)
             )
+
+        make_identity(nc, ident[:])
+        pw_bank = bank(PW_BANK, "pw_bank")
+        pw_turned = sb("pw_turned", [P, P], F32)
+        nc.tensor.transpose(pw_bank[:, P : 2 * P], pw_pad[:], ident[:])
+        nc.scalar.copy(pw_turned[:], pw_bank[:, P : 2 * P])
+        nc.tensor.transpose(pw_bank[:, 0:P], pw_turned[:], ident[:])
+        pw_psum = pw_bank[:, 0 : M_PASSES * PACK].rearrange("p (b t) -> p b t", t=PACK)
 
         def deal(dst, src, walk):
             nc.vector.tensor_copy(
@@ -115,7 +130,7 @@ def tile_list_prior_art_expansion_kernel(
 
         def gather_patents(b):
             entries = list2[:, b * KP // LIST_ROWS : (b + 1) * KP // LIST_ROWS]
-            v2_codes[b] = keep.tile([P, KP], U32, name="v2_codes%d" % b, tag="h_bf0" if b else "v2_first", align_bytes=64)
+            v2_codes[b] = sb("v2_codes%d" % b, [P, KP], U32)
             dealt = v2_codes[b][:].rearrange("p (t m) -> p m t", t=PACK)
             nc.vector.tensor_copy(dealt, t2_words[:].bitcast(U32).indirect(entries))
 
@@ -155,58 +170,66 @@ def tile_list_prior_art_expansion_kernel(
 
         chunks = len(WIDTHS)
         starts = [sum(WIDTHS[:c]) for c in range(chunks)]
-        def outputs_in(banks, width):
-            per_bank = PACK // len(banks)
-            return [banks[t // per_bank][:, (t % per_bank) * width : (t % per_bank + 1) * width] for t in range(PACK)]
-
+        groups = S // H_WIDTH
         h_psum = {}
 
-        def first_product(c, a):
-            per_bank = PACK // len(H_BANKS[c])
-            cols = slice(starts[c], starts[c] + WIDTHS[c])
+        def first_product(g, half, a):
+            cols = slice(g * H_WIDTH, (g + 1) * H_WIDTH)
             if a == 0:
-                h_psum[c] = outputs_in([bank(k, "h%d_%d" % (c, k)) for k in H_BANKS[c]], WIDTHS[c])
-            for t in range(PACK):
+                h_psum[g, half] = bank(H_BANKS[g][half], "h%d_%d" % (g, half))
+            for i in range(2):
+                t = 2 * half + i
                 nc.tensor.matmul_mx(
-                    h_psum[c][t],
+                    h_psum[g, half][:, i * H_WIDTH : (i + 1) * H_WIDTH],
                     lhsT=w_codes[a][:, t * P : (t + 1) * P].bitcast(FP8X4),
                     lhsT_scale=w_scales[a][:, t * P : (t + 1) * P],
                     rhs=v_codes[a][:, cols].bitcast(FP8X4),
                     rhs_scale=v_scales[V_SCALE_ROW + 4 * a : P, cols],
-                    start=(a == 0 and t % per_bank == 0),
-                    stop=(a == K_PASSES - 1 and t % per_bank == per_bank - 1),
+                    start=(a == 0 and i == 0),
+                    stop=(a == K_PASSES - 1 and i == 1),
                 )
 
-        h = [sb("h%d" % c, [P, PACK, w], F32) for c, w in enumerate(WIDTHS)]
-        h_bf = [sb("h_bf%d" % c, [P, w, PACK], BF16) for c, w in enumerate(WIDTHS)]
-        h_codes = [sb("h_codes%d" % c, [P, w], U32) for c, w in enumerate(WIDTHS)]
-        h_scales = [sb("h_scales%d" % c, [P, w], U8) for c, w in enumerate(WIDTHS)]
+        h = [sb("h%d" % g, [P, PACK, H_WIDTH], F32) for g in range(groups)]
+        h_codes = sb("h_codes", [P, S], U32)
+        h_scales = [sb("h_scales%d" % g, [P, H_WIDTH], U8) for g in range(groups)]
 
-        def h_of(c):
-            return h[c][:]
+        d_at = []
+        end = PACK * H_WIDTH
+        for c, w in enumerate(WIDTHS):
+            d_at.append(end - (OVERLAP if GPSIMD_CLAIMS[c] else 0))
+            end = d_at[c] + M_PASSES * PACK * w
+        staged = sb("staged", [P, end], BF16)
+        h_bf = [sb("h_bf%d" % g, [P, H_WIDTH * PACK], BF16)[:] for g in range(groups - 1)] + [staged[:, 0 : PACK * H_WIDTH]]
 
-        def h_out(c):
+        def h_out(g):
             for t in range(PACK):
-                nc.scalar.activation(h[c][:, t, :], h_psum[c][t], ACT.Identity, bias=bq_t[:, t : t + 1])
+                summed = h_psum[g, t // 2][:, (t % 2) * H_WIDTH : (t % 2 + 1) * H_WIDTH]
+                if g == groups - 1:
+                    nc.vector.tensor_scalar_add(h[g][:, t, :], summed, bq_t[:, t : t + 1])
+                else:
+                    nc.scalar.activation(h[g][:, t, :], summed, ACT.Identity, bias=bq_t[:, t : t + 1])
 
-        def h_round(c):
-            copy = nc.vector.tensor_copy if c in ROUND_ON_VECTOR else nc.scalar.copy
-            copy(h_bf[c][:].rearrange("p (n i) t -> p n t i", i=PACK), h_of(c).rearrange("p t (n i) -> p n t i", i=PACK))
+        def h_round(g):
+            if g == 0:
+                nc.gpsimd.tensor_scalar(
+                    h_bf[g].rearrange("p (n t) -> p n t", t=PACK), h[g][:].rearrange("p t n -> p n t"), 1.0, 0.0, ALU.mult, ALU.add
+                )
+                return
+            nc.vector.tensor_copy(
+                h_bf[g].rearrange("p (n i t) -> p n t i", i=PACK, t=PACK), h[g][:].rearrange("p t (n i) -> p n t i", i=PACK)
+            )
 
-        def h_quantize(c):
-            nc.vector.quantize_mx(h_codes[c][:].bitcast(FP8X4), h_scales[c][:], h_bf[c][:].rearrange("p n t -> p (n t)"))
+        def h_quantize(g):
+            nc.vector.quantize_mx(h_codes[:, g * H_WIDTH : (g + 1) * H_WIDTH].bitcast(FP8X4), h_scales[g][:], h_bf[g])
 
         gate = {}
-        d_bf = [sb("d_bf%d" % c, [P, M_PASSES * w * PACK], BF16) for c, w in enumerate(WIDTHS)]
         d_codes = [sb("d_codes%d" % c, [P, M_PASSES * w], U32) for c, w in enumerate(WIDTHS)]
         d_scales = [sb("d_scales%d" % c, [P, M_PASSES * w], U8) for c, w in enumerate(WIDTHS)]
 
         def second_product(c, b):
-            gate[c, b] = keep.tile(
-                [P, WIDTHS[c] * PACK], F32, name="gate%d_%d" % (c, b), tag="gate", bufs=GATE_BUFS, align_bytes=64
-            )
+            gate[c, b] = sb("gate%d_%d" % (c, b), [P, WIDTHS[c] * PACK], F32)
             for u in range(WIDTHS[c] // SUB):
-                cols = slice(u * SUB, (u + 1) * SUB)
+                j0 = starts[c] + u * SUB
                 turn = (M_PASSES * starts[c] + b * WIDTHS[c]) // SUB + u
                 e = bank(E_BANKS[turn % len(E_BANKS)], "e%d" % turn)
                 for t in range(PACK):
@@ -215,8 +238,8 @@ def tile_list_prior_art_expansion_kernel(
                         e[:, t * SUB : (t + 1) * SUB],
                         lhsT=v2_codes[b][:, t * P : (t + 1) * P].bitcast(FP8X4),
                         lhsT_scale=v2_scales[:, m],
-                        rhs=h_codes[c][:, cols].bitcast(FP8X4),
-                        rhs_scale=h_scales[c][:, cols],
+                        rhs=h_codes[:, j0 : j0 + SUB].bitcast(FP8X4),
+                        rhs_scale=h_scales[j0 // H_WIDTH][:, j0 % H_WIDTH : j0 % H_WIDTH + SUB],
                         start=True,
                         stop=True,
                     )
@@ -229,6 +252,18 @@ def tile_list_prior_art_expansion_kernel(
                         ACT.Sigmoid,
                     )
 
+        def d_bf(c, b, n0, n1):
+            first = d_at[c] + b * WIDTHS[c] * PACK
+            return staged[:, first + n0 * PACK : first + n1 * PACK]
+
+        def weigh_claims(engine, weights, c, b, n0, n1):
+            engine.tensor_tensor(
+                d_bf(c, b, n0, n1).rearrange("p (n t) -> p n t", t=PACK),
+                gate[c, b][:, n0 * PACK : n1 * PACK].rearrange("p (n t) -> p n t", t=PACK),
+                weights[:, b, :].unsqueeze(1).to_broadcast([P, n1 - n0, PACK]),
+                ALU.mult,
+            )
+
         def weigh(c, b):
             w = WIDTHS[c]
             if (c, b) in WEIGH_ON_SCALAR:
@@ -239,101 +274,91 @@ def tile_list_prior_art_expansion_kernel(
                         rows[:, t, :].rearrange("p (u n) -> p u n", n=SUB), by_t[:, t], ACT.Copy, scale=pw_t[:, b, t : t + 1]
                     )
                 nc.scalar.copy(
-                    d_bf[c][:, b * w * PACK : (b + 1) * w * PACK].rearrange("p (n i t) -> p n t i", i=PACK, t=PACK),
+                    d_bf(c, b, 0, w).rearrange("p (n i t) -> p n t i", i=PACK, t=PACK),
                     rows[:].rearrange("p t (n i) -> p n t i", i=PACK),
                 )
                 return
-            nc.vector.tensor_tensor(
-                d_bf[c][:, b * w * PACK : (b + 1) * w * PACK].rearrange("p (n t) -> p n t", t=PACK),
-                gate[c, b][:].rearrange("p (n t) -> p n t", t=PACK),
-                pw_t[:, b, :].unsqueeze(1).to_broadcast([P, w, PACK]),
-                ALU.mult,
-            )
+            shared = GPSIMD_CLAIMS[c] if b == 0 else 0
+            if shared:
+                weigh_claims(nc.gpsimd, pw_t, c, b, 0, shared)
+            if shared < w:
+                weigh_claims(nc.vector, pw_psum, c, b, shared, w)
+
+        def d_quantize(c):
+            w = WIDTHS[c]
+            nc.vector.quantize_mx(d_codes[c][:].bitcast(FP8X4), d_scales[c][:], staged[:, d_at[c] : d_at[c] + M_PASSES * PACK * w])
 
         x_psum = {}
 
-        def d_quantize(c, b0, b1):
+        def third_product(c):
             w = WIDTHS[c]
-            cols = slice(b0 * w, b1 * w)
-            nc.vector.quantize_mx(
-                d_codes[c][:, cols].bitcast(FP8X4), d_scales[c][:, cols], d_bf[c][:, b0 * w * PACK : b1 * w * PACK]
-            )
-
-        def third_product(c, b):
-            w = WIDTHS[c]
-            per_bank = PACK // len(X_BANKS[c])
-            if b == 0:
-                banks = [bank(k, "x%d_%d" % (c, k)) for k in X_BANKS[c]]
-                x_psum[c] = [banks[t // per_bank][:, (t % per_bank) * w : (t % per_bank + 1) * w] for t in range(PACK)]
-            for t in range(PACK):
-                n0 = b * H + t * P
-                for u in range(w // SUB):
-                    cols = slice(b * w + u * SUB, b * w + (u + 1) * SUB)
-                    nc.tensor.matmul_mx(
-                        x_psum[c][t][:, u * SUB : (u + 1) * SUB],
-                        lhsT=vm_codes[:, 2 * n0 : 2 * (n0 + P)].bitcast(FP4X4),
-                        lhsT_scale=vm_dealt_scales[:, n0 : n0 + P],
-                        rhs=d_codes[c][:, cols].bitcast(FP8X4),
-                        rhs_scale=d_scales[c][:, cols],
-                        start=(b == 0 and t % per_bank == 0 and u == 0),
-                        stop=(b == M_PASSES - 1 and t % per_bank == per_bank - 1 and u == w // SUB - 1),
-                    )
+            for half in range(2):
+                x_psum[c, half] = bank(X_BANKS[c][half], "x%d_%d" % (c, half))
+                for b in range(M_PASSES):
+                    for i in range(2):
+                        n0 = b * H + (2 * half + i) * P
+                        for u in range(w // SUB):
+                            cols = slice(b * w + u * SUB, b * w + (u + 1) * SUB)
+                            nc.tensor.matmul_mx(
+                                x_psum[c, half][:, i * w + u * SUB : i * w + (u + 1) * SUB],
+                                lhsT=vm_codes[:, 2 * n0 : 2 * (n0 + P)].bitcast(FP4X4),
+                                lhsT_scale=vm_dealt_scales[:, n0 : n0 + P],
+                                rhs=d_codes[c][:, cols].bitcast(FP8X4),
+                                rhs_scale=d_scales[c][:, cols],
+                                start=(b == 0 and i == 0 and u == 0),
+                                stop=(b == M_PASSES - 1 and i == 1 and u == w // SUB - 1),
+                            )
 
         out_rows = out.rearrange("(p t) j -> p t j", t=PACK)
 
-        def finish(c, half):
-            ts = slice(2 * half, 2 * half + 2)
-            for t in range(ts.start, ts.stop):
-                nc.vector.scalar_tensor_tensor(h[c][:, t, :], h[c][:, t, :], rg_t[:, t : t + 1], x_psum[c][t], ALU.mult, ALU.add)
-            nc.sync.dma_start(out_rows[:, ts, starts[c] : starts[c] + WIDTHS[c]], h[c][:, ts, :])
+        def finish(c):
+            w = WIDTHS[c]
+            g, j0 = divmod(starts[c], H_WIDTH)
+            for half in range(2):
+                for i in range(2):
+                    t = 2 * half + i
+                    kept = h[g][:, t, j0 : j0 + w]
+                    nc.vector.scalar_tensor_tensor(
+                        kept, kept, rg_t[:, t : t + 1], x_psum[c, half][:, i * w : (i + 1) * w], ALU.mult, ALU.add
+                    )
+                ts = slice(2 * half, 2 * half + 2)
+                nc.sync.dma_start(out_rows[:, ts, starts[c] : starts[c] + w], h[g][:, ts, j0 : j0 + w])
 
+        early = [(g, half) for g in range(groups) for half in range(2)][:-1]
         for a in range(K_PASSES - 1):
-            for c in range(chunks):
-                first_product(c, a)
+            for g, half in early:
+                first_product(g, half, a)
         gather_words(K_PASSES - 1, 0, S // 2)
         gather_words(K_PASSES - 1, S // 2, S)
-        for c in range(chunks):
-            first_product(c, K_PASSES - 1)
+        for g, half in early:
+            first_product(g, half, K_PASSES - 1)
         h_out(0)
-        gather_patents(0)
+        for a in range(K_PASSES):
+            first_product(groups - 1, 1, a)
         h_round(0)
+        gather_patents(0)
+        gather_patents(1)
         h_quantize(0)
         h_out(1)
-        gather_patents(1)
-        second_product(0, 0)
+        h_out(2)
         h_round(1)
+        h_out(3)
         h_quantize(1)
-        for c in range(2, 4):
-            h_out(c)
-        second_product(0, 1)
-        last = chunks - 1
+        h_round(2)
+        h_round(3)
+        h_quantize(2)
+        h_quantize(3)
+        for c in range(AHEAD):
+            for b in range(M_PASSES):
+                second_product(c, b)
         for c in range(chunks):
-            if c + 4 <= last:
-                h_out(c + 4)
-            if c + 1 <= last:
-                second_product(c + 1, 0)
-            if c + 2 <= last:
-                h_round(c + 2)
-            if c + 1 <= last:
-                second_product(c + 1, 1)
-            weigh(c, 0)
-            if c + 2 <= last:
-                h_quantize(c + 2)
-            if c == last:
-                finish(c - 1, 0)
-                d_quantize(c, 0, 1)
-                third_product(c, 0)
-            weigh(c, 1)
-            if 0 < c < last:
-                finish(c - 1, 0)
-            if c == last:
-                finish(c - 1, 1)
-                d_quantize(c, 1, 2)
-            else:
-                d_quantize(c, 0, M_PASSES)
-                third_product(c, 0)
-            third_product(c, 1)
-            if 0 < c < last:
-                finish(c - 1, 1)
-        finish(last, 0)
-        finish(last, 1)
+            if c + AHEAD < chunks:
+                for b in range(M_PASSES):
+                    second_product(c + AHEAD, b)
+            for b in range(M_PASSES):
+                weigh(c, b)
+            d_quantize(c)
+            if c > 0:
+                finish(c - 1)
+            third_product(c)
+        finish(chunks - 1)

@@ -28,14 +28,13 @@ SUB = P
 V_SCALE_ROW = 4
 
 H_WIDTH = 256
-H_BANKS = ((0, 1), (2, 3), (4, 5), (6, 0))
-E_BANKS = (1, 2, 3)
+H_BANKS = ((0, 1), (2, 3), (4, 5), (0, 1))
+E_BANKS = (6, 2, 3)
 PW_BANK = 7
 WIDTHS = (256, 256, 256, 128, 128)
-X_BANKS = ((4, 5), (6, 0), (4, 5), (6, 0), (4, 5))
-GPSIMD_CLAIMS = (128, 192, 192, 128, 0)
-WEIGH_ON_SCALAR = ((3, 1), (4, 1))
-AHEAD = 2
+X_BANKS = ((4, 5), (0, 1), (4, 5), (0, 1), (4, 5))
+GPSIMD_CLAIMS = (128, 128, 128, 128, 0)
+WEIGH_ON_SCALAR = ((3, 1), (4, 0), (4, 1))
 OVERLAP = 32
 
 
@@ -199,7 +198,10 @@ def tile_list_prior_art_expansion_kernel(
             d_at.append(end - (OVERLAP if GPSIMD_CLAIMS[c] else 0))
             end = d_at[c] + M_PASSES * PACK * w
         staged = sb("staged", [P, end], BF16)
-        h_bf = [sb("h_bf%d" % g, [P, H_WIDTH * PACK], BF16)[:] for g in range(groups - 1)] + [staged[:, 0 : PACK * H_WIDTH]]
+        h_bf = [
+            staged[:, 0 : PACK * H_WIDTH] if g == groups - 2 else sb("h_bf%d" % g, [P, H_WIDTH * PACK], BF16)[:]
+            for g in range(groups)
+        ]
 
         def h_out(g):
             for t in range(PACK):
@@ -210,12 +212,8 @@ def tile_list_prior_art_expansion_kernel(
                     nc.scalar.activation(h[g][:, t, :], summed, ACT.Identity, bias=bq_t[:, t : t + 1])
 
         def h_round(g):
-            if g == 0:
-                nc.gpsimd.tensor_scalar(
-                    h_bf[g].rearrange("p (n t) -> p n t", t=PACK), h[g][:].rearrange("p t n -> p n t"), 1.0, 0.0, ALU.mult, ALU.add
-                )
-                return
-            nc.vector.tensor_copy(
+            copy = nc.scalar.copy if g == 0 else nc.vector.tensor_copy
+            copy(
                 h_bf[g].rearrange("p (n i t) -> p n t i", i=PACK, t=PACK), h[g][:].rearrange("p t (n i) -> p n t i", i=PACK)
             )
 
@@ -324,7 +322,7 @@ def tile_list_prior_art_expansion_kernel(
                 ts = slice(2 * half, 2 * half + 2)
                 nc.sync.dma_start(out_rows[:, ts, starts[c] : starts[c] + w], h[g][:, ts, j0 : j0 + w])
 
-        early = [(g, half) for g in range(groups) for half in range(2)][:-1]
+        early = [(g, half) for g in range(groups - 1) for half in range(2)]
         for a in range(K_PASSES - 1):
             for g, half in early:
                 first_product(g, half, a)
@@ -333,28 +331,25 @@ def tile_list_prior_art_expansion_kernel(
         for g, half in early:
             first_product(g, half, K_PASSES - 1)
         h_out(0)
-        for a in range(K_PASSES):
-            first_product(groups - 1, 1, a)
+        for half in range(2):
+            for a in range(K_PASSES):
+                first_product(groups - 1, half, a)
         h_round(0)
         gather_patents(0)
         gather_patents(1)
         h_quantize(0)
-        h_out(1)
-        h_out(2)
+        for g in range(1, groups):
+            h_out(g)
         h_round(1)
-        h_out(3)
+        h_round(3)
         h_quantize(1)
         h_round(2)
-        h_round(3)
-        h_quantize(2)
         h_quantize(3)
-        for c in range(AHEAD):
+        h_quantize(2)
+        for c in range(chunks):
             for b in range(M_PASSES):
                 second_product(c, b)
         for c in range(chunks):
-            if c + AHEAD < chunks:
-                for b in range(M_PASSES):
-                    second_product(c + AHEAD, b)
             for b in range(M_PASSES):
                 weigh(c, b)
             d_quantize(c)

@@ -32,9 +32,9 @@ H_BANKS = ((0, 1), (2, 3), (4, 5), (0, 1))
 E_BANKS = (6, 2, 3)
 PW_BANK = 7
 WIDTHS = (256, 256, 256, 128, 128)
-X_BANKS = ((4, 5), (0, 1), (4, 5), (0, 1), (4, 5))
-GPSIMD_CLAIMS = (128, 128, 128, 128, 0)
-WEIGH_ON_SCALAR = ((3, 1), (4, 0), (4, 1))
+X_BANKS = ((4, 5), (0, 1), (4, 5), (0, 1), (2, 3))
+GPSIMD_CLAIMS = (176, 0, 128, 128, 128)
+SCALAR_CLAIMS = (0, 0, 96, 128, 128)
 OVERLAP = 32
 
 
@@ -193,11 +193,12 @@ def tile_list_prior_art_expansion_kernel(
         h_scales = [sb("h_scales%d" % g, [P, H_WIDTH], U8) for g in range(groups)]
 
         d_at = []
-        end = PACK * H_WIDTH
+        end = [PACK * H_WIDTH, 0]
         for c, w in enumerate(WIDTHS):
-            d_at.append(end - (OVERLAP if GPSIMD_CLAIMS[c] else 0))
-            end = d_at[c] + M_PASSES * PACK * w
-        staged = sb("staged", [P, end], BF16)
+            d_at.append(end[c % 2] - (OVERLAP if GPSIMD_CLAIMS[c] else 0))
+            end[c % 2] = d_at[c] + M_PASSES * PACK * w
+        rounded = [sb("rounded%d" % k, [P, end[k]], BF16) for k in range(2)]
+        staged = rounded[0]
         h_bf = [
             staged[:, 0 : PACK * H_WIDTH] if g == groups - 2 else sb("h_bf%d" % g, [P, H_WIDTH * PACK], BF16)[:]
             for g in range(groups)
@@ -241,18 +242,25 @@ def tile_list_prior_art_expansion_kernel(
                         start=True,
                         stop=True,
                     )
-                if (c, b) in WEIGH_ON_SCALAR:
-                    nc.scalar.activation(gate[c, b][:, u * KP : (u + 1) * KP], e[:], ACT.Sigmoid)
-                else:
+                rows = SCALAR_CLAIMS[c] if b == M_PASSES - 1 and u == WIDTHS[c] // SUB - 1 else 0
+                woven = SUB - rows
+                by_t = e[:].rearrange("p (t n) -> p t n", t=PACK)
+                if woven:
                     nc.scalar.activation(
-                        gate[c, b][:, u * KP : (u + 1) * KP].rearrange("p (n t) -> p n t", t=PACK),
-                        e[:].rearrange("p (t n) -> p n t", t=PACK),
+                        gate[c, b][:, u * KP : u * KP + woven * PACK].rearrange("p (n t) -> p n t", t=PACK),
+                        by_t[:, :, 0:woven].rearrange("p t n -> p n t"),
+                        ACT.Sigmoid,
+                    )
+                if rows:
+                    nc.scalar.activation(
+                        gate[c, b][:, u * KP + woven * PACK : (u + 1) * KP].rearrange("p (t n) -> p t n", t=PACK),
+                        by_t[:, :, woven:SUB],
                         ACT.Sigmoid,
                     )
 
         def d_bf(c, b, n0, n1):
             first = d_at[c] + b * WIDTHS[c] * PACK
-            return staged[:, first + n0 * PACK : first + n1 * PACK]
+            return rounded[c % 2][:, first + n0 * PACK : first + n1 * PACK]
 
         def weigh_claims(engine, weights, c, b, n0, n1):
             engine.tensor_tensor(
@@ -262,37 +270,40 @@ def tile_list_prior_art_expansion_kernel(
                 ALU.mult,
             )
 
-        def weigh(c, b):
-            w = WIDTHS[c]
-            if (c, b) in WEIGH_ON_SCALAR:
-                rows = sb("d_rows%d_%d" % (c, b), [P, PACK, w], BF16)
-                by_t = gate[c, b][:].rearrange("p (u t n) -> p t u n", t=PACK, n=SUB)
-                for t in range(PACK):
-                    nc.scalar.activation(
-                        rows[:, t, :].rearrange("p (u n) -> p u n", n=SUB), by_t[:, t], ACT.Copy, scale=pw_t[:, b, t : t + 1]
-                    )
-                nc.scalar.copy(
-                    d_bf(c, b, 0, w).rearrange("p (n i t) -> p n t i", i=PACK, t=PACK),
-                    rows[:].rearrange("p t (n i) -> p n t i", i=PACK),
-                )
-                return
-            shared = GPSIMD_CLAIMS[c] if b == 0 else 0
-            if shared:
-                weigh_claims(nc.gpsimd, pw_t, c, b, 0, shared)
-            if shared < w:
-                weigh_claims(nc.vector, pw_psum, c, b, shared, w)
+        def weigh_on_scalar(c, b):
+            w, n = WIDTHS[c], SCALAR_CLAIMS[c]
+            rows = sb("d_rows%d_%d" % (c, b), [P, PACK, n], BF16)
+            by_t = gate[c, b][:, (w - n) * PACK :].rearrange("p (t n) -> p t n", t=PACK)
+            for t in range(PACK):
+                nc.scalar.activation(rows[:, t, :], by_t[:, t, :], ACT.Copy, scale=pw_t[:, b, t : t + 1])
+            nc.scalar.copy(
+                d_bf(c, b, w - n, w).rearrange("p (n i t) -> p n t i", i=PACK, t=PACK),
+                rows[:].rearrange("p t (n i) -> p n t i", i=PACK),
+            )
 
-        def d_quantize(c):
+        def weigh(c, b):
+            first = GPSIMD_CLAIMS[c] if b == 0 else 0
+            last = WIDTHS[c] - (SCALAR_CLAIMS[c] if b == M_PASSES - 1 else 0)
+            if first:
+                weigh_claims(nc.gpsimd, pw_t, c, b, 0, first)
+            if first < last:
+                weigh_claims(nc.vector, pw_psum, c, b, first, last)
+
+        def d_quantize(c, b0, b1):
             w = WIDTHS[c]
-            nc.vector.quantize_mx(d_codes[c][:].bitcast(FP8X4), d_scales[c][:], staged[:, d_at[c] : d_at[c] + M_PASSES * PACK * w])
+            cols = slice(b0 * w, b1 * w)
+            nc.vector.quantize_mx(
+                d_codes[c][:, cols].bitcast(FP8X4), d_scales[c][:, cols], rounded[c % 2][:, d_at[c] + b0 * PACK * w : d_at[c] + b1 * PACK * w]
+            )
 
         x_psum = {}
 
-        def third_product(c):
+        def third_product(c, passes):
             w = WIDTHS[c]
             for half in range(2):
-                x_psum[c, half] = bank(X_BANKS[c][half], "x%d_%d" % (c, half))
-                for b in range(M_PASSES):
+                for b in passes:
+                    if b == 0:
+                        x_psum[c, half] = bank(X_BANKS[c][half], "x%d_%d" % (c, half))
                     for i in range(2):
                         n0 = b * H + (2 * half + i) * P
                         for u in range(w // SUB):
@@ -349,11 +360,21 @@ def tile_list_prior_art_expansion_kernel(
         for c in range(chunks):
             for b in range(M_PASSES):
                 second_product(c, b)
-        for c in range(chunks):
+                if (c, b) == (3, 0):
+                    weigh_on_scalar(2, 1)
+        weigh_on_scalar(3, 1)
+        weigh_on_scalar(4, 1)
+        last = chunks - 1
+        for c in range(last):
             for b in range(M_PASSES):
                 weigh(c, b)
-            d_quantize(c)
+            d_quantize(c, 0, M_PASSES)
             if c > 0:
                 finish(c - 1)
-            third_product(c)
-        finish(chunks - 1)
+            third_product(c, range(M_PASSES))
+        for b in range(M_PASSES):
+            weigh(last, b)
+            d_quantize(last, b, b + 1)
+            third_product(last, [b])
+        finish(last - 1)
+        finish(last)

@@ -59,8 +59,8 @@ def tile_list_prior_art_expansion_kernel(
         t_words = [sb("t_words%d" % a, [P, T], I32) for a in range(K_PASSES)]
         t_scales = sb("t_scales", [P, T], U8)
         w_raw = [sb("w_raw%d" % a, [P, PACK, H], F32) for a in range(K_PASSES)]
-        vm_raw = sb("vm_raw", [P, M_PASSES, H // 2], I32)
-        vm_raw_scales = sb("vm_raw_scales", [P, M_PASSES * H], U8)
+        vm_codes = sb("vm_codes", [P, M_PASSES * H * 2], U8)
+        vm_planes = sb("vm_planes", [P, M_PASSES * H], U8)
         bq_t = sb("bq_t", [P, PACK], F32)
         rg_t = sb("rg_t", [P, PACK], F32)
         pw_pad = sb("pw_pad", [P, P], F32)
@@ -70,7 +70,7 @@ def tile_list_prior_art_expansion_kernel(
 
         nc.gpsimd.memset(t2_scales[:].bitcast(I32), 0)
         nc.vector.memset(t_scales[:].bitcast(I32), 0)
-        nc.gpsimd.memset(vm_raw_scales[:].bitcast(I32), 0)
+        nc.gpsimd.memset(vm_planes[:].bitcast(I32), 0)
         nc.gpsimd.memset(pw_pad[:], 0.0)
         nc.gpsimd.memset(warm[:, 0:1], 0.0)
         nc.scalar.activation(warm[:, 1:2], warm[:, 0:1], ACT.Sigmoid)
@@ -89,18 +89,21 @@ def tile_list_prior_art_expansion_kernel(
         for r in range(PACK):
             nc.sync.dma_start(t2_scales[r:P:32, :].bitcast(I32), tab2_scales[0, r:16:4, :].bitcast(I32))
         load_w(1)
-        nc.sync.dma_start(vm_raw[:], vm_words.rearrange("b p n -> p b n").bitcast(I32))
         load_w(2)
-        for r in range(PACK):
-            nc.sync.dma_start(
-                vm_raw_scales[r:P:32, :].bitcast(I32).rearrange("q (b n) -> q b n", b=M_PASSES),
-                vm_scales[:, r:16:4, :].rearrange("b q n -> q b n").bitcast(I32),
-            )
         nc.sync.dma_start(pw_t, pw.rearrange("(b p t) -> p b t", b=M_PASSES, t=PACK))
         load_words(t_words[1], tab_words, 1)
         load_words(t_words[2], tab_words, 2)
         load_words(t2_words, tab2_words, 0)
-        nc.sync.dma_start(rg_t[:], rg.rearrange("(p t) -> p t", t=PACK))
+        nc.sync.dma_start(
+            vm_codes[:].bitcast(I32).rearrange("p (b n) -> p b n", b=M_PASSES), vm_words.rearrange("b p n -> p b n").bitcast(I32)
+        )
+        for r in range(PACK):
+            nc.sync.dma_start(
+                vm_planes[r:P:32, :].bitcast(I32).rearrange("q (b n) -> q b n", b=M_PASSES),
+                vm_scales[:, r:16:4, :].rearrange("b q n -> q b n").bitcast(I32),
+            )
+        with nc.allow_non_contiguous_dma(reason="one gain for each partition and output"):
+            nc.sync.dma_start(rg_t[:], rg.rearrange("(t p) -> p t", t=PACK))
         for q in range(QUADS):
             first = 32 * q + V_SCALE_ROW
             nc.gpsimd.dma_start(
@@ -152,17 +155,12 @@ def tile_list_prior_art_expansion_kernel(
         def w_quantize(a):
             nc.vector.quantize_mx(w_codes[a][:].bitcast(FP8X4), w_scales[a][:], w_bf[a][:])
 
-        vm_codes = sb("vm_codes", [P, M_PASSES * H * 2], U8)
-        vm_dealt_scales = sb("vm_dealt_scales", [P, M_PASSES * H], U8)
-
         gather_words(0, 0, S)
         nc.vector.tensor_copy(v_scales[:], t_scales[:].indirect(list1[:]))
         w_quantize(0)
         nc.vector.tensor_copy(v2_picked_scales[:], t2_scales[:].indirect(list2[:]))
         w_quantize(1)
         deal(v2_scales[:], v2_picked_scales[:], write_in_order)
-        deal(vm_codes[:].bitcast(U16), vm_raw[:].rearrange("p b n -> p (b n)").bitcast(U16), write_in_order)
-        deal(vm_dealt_scales[:], vm_raw_scales[:], write_in_order)
         w_quantize(2)
         gather_words(1, 0, S // 2)
         gather_words(1, S // 2, S)
@@ -189,6 +187,7 @@ def tile_list_prior_art_expansion_kernel(
                 )
 
         h = [sb("h%d" % g, [P, PACK, H_WIDTH], F32) for g in range(groups)]
+        kept_h = [sb("kept_h%d" % g, [P, PACK, H_WIDTH], F32) for g in range(groups)]
         h_codes = sb("h_codes", [P, S], U32)
         h_scales = [sb("h_scales%d" % g, [P, H_WIDTH], U8) for g in range(groups)]
 
@@ -211,6 +210,10 @@ def tile_list_prior_art_expansion_kernel(
                     nc.vector.tensor_scalar_add(h[g][:, t, :], summed, bq_t[:, t : t + 1])
                 else:
                     nc.scalar.activation(h[g][:, t, :], summed, ACT.Identity, bias=bq_t[:, t : t + 1])
+
+        def h_keep(g):
+            for q in range(QUADS):
+                nc.sync.dma_start(kept_h[g][:, q, :], h[g][32 * q : 32 * (q + 1), :, :])
 
         def h_round(g):
             copy = nc.scalar.copy if g == 0 else nc.vector.tensor_copy
@@ -311,14 +314,14 @@ def tile_list_prior_art_expansion_kernel(
                             nc.tensor.matmul_mx(
                                 x_psum[c, half][:, i * w + u * SUB : i * w + (u + 1) * SUB],
                                 lhsT=vm_codes[:, 2 * n0 : 2 * (n0 + P)].bitcast(FP4X4),
-                                lhsT_scale=vm_dealt_scales[:, n0 : n0 + P],
+                                lhsT_scale=vm_planes[:, n0 : n0 + P],
                                 rhs=d_codes[c][:, cols].bitcast(FP8X4),
                                 rhs_scale=d_scales[c][:, cols],
                                 start=(b == 0 and i == 0 and u == 0),
                                 stop=(b == M_PASSES - 1 and i == 1 and u == w // SUB - 1),
                             )
 
-        out_rows = out.rearrange("(p t) j -> p t j", t=PACK)
+        out_rows = out.rearrange("(t p) j -> p t j", t=PACK)
 
         def finish(c):
             w = WIDTHS[c]
@@ -326,12 +329,12 @@ def tile_list_prior_art_expansion_kernel(
             for half in range(2):
                 for i in range(2):
                     t = 2 * half + i
-                    kept = h[g][:, t, j0 : j0 + w]
+                    kept = kept_h[g][:, t, j0 : j0 + w]
                     nc.vector.scalar_tensor_tensor(
                         kept, kept, rg_t[:, t : t + 1], x_psum[c, half][:, i * w : (i + 1) * w], ALU.mult, ALU.add
                     )
                 ts = slice(2 * half, 2 * half + 2)
-                nc.sync.dma_start(out_rows[:, ts, starts[c] : starts[c] + w], h[g][:, ts, j0 : j0 + w])
+                nc.sync.dma_start(out_rows[:, ts, starts[c] : starts[c] + w], kept_h[g][:, ts, j0 : j0 + w])
 
         early = [(g, half) for g in range(groups - 1) for half in range(2)]
         for a in range(K_PASSES - 1):
@@ -351,6 +354,8 @@ def tile_list_prior_art_expansion_kernel(
         h_quantize(0)
         for g in range(1, groups):
             h_out(g)
+        for g in range(groups):
+            h_keep(g)
         h_round(1)
         h_round(3)
         h_quantize(1)

@@ -84,12 +84,14 @@ def tile_list_prior_art_expansion_kernel(
         nc.sync.dma_start(list1[:], offs)
         load_words(t_words[0], tab_words, 0)
         load_w(0)
-        nc.sync.dma_start(bq_t[:], bq.rearrange("(p t) -> p t", t=PACK))
         nc.sync.dma_start(list2[:], offs2)
         for r in range(PACK):
             nc.sync.dma_start(t2_scales[r:P:32, :].bitcast(I32), tab2_scales[0, r:16:4, :].bitcast(I32))
-        load_w(1)
+        halves = wq[KP : 2 * KP, :].rearrange("(p i) r -> p i r", i=PACK)
+        nc.sync.dma_start(w_raw[1][:, 0:2, :], halves[:, 0:2, :])
+        nc.sync.dma_start(w_raw[1][:, 2:PACK, :], halves[:, 2:PACK, :])
         load_w(2)
+        nc.sync.dma_start(bq_t[:], bq.rearrange("(p t) -> p t", t=PACK))
         nc.sync.dma_start(pw_t, pw.rearrange("(b p t) -> p b t", b=M_PASSES, t=PACK))
         load_words(t_words[1], tab_words, 1)
         load_words(t_words[2], tab_words, 2)

@@ -35,6 +35,7 @@ WIDTHS = (256, 256, 256, 128, 128)
 X_BANKS = ((4, 5), (0, 1), (4, 5), (0, 1), (2, 3))
 GPSIMD_CLAIMS = (176, 0, 128, 128, 128)
 SCALAR_CLAIMS = (0, 0, 96, 128, 128)
+ASIDE = 16
 OVERLAP = 32
 
 
@@ -85,14 +86,13 @@ def tile_list_prior_art_expansion_kernel(
         load_words(t_words[0], tab_words, 0)
         load_w(0)
         nc.sync.dma_start(list2[:], offs2)
-        for r in range(PACK):
-            nc.sync.dma_start(t2_scales[r:P:32, :].bitcast(I32), tab2_scales[0, r:16:4, :].bitcast(I32))
+        nc.sync.dma_start(t2_scales[ASIDE : 2 * ASIDE, :].bitcast(I32), tab2_scales[0].bitcast(I32))
+        nc.sync.dma_start(bq_t[:], bq.rearrange("(p t) -> p t", t=PACK))
+        nc.sync.dma_start(pw_t, pw.rearrange("(b p t) -> p b t", b=M_PASSES, t=PACK))
         halves = wq[KP : 2 * KP, :].rearrange("(p i) r -> p i r", i=PACK)
         nc.sync.dma_start(w_raw[1][:, 0:2, :], halves[:, 0:2, :])
         nc.sync.dma_start(w_raw[1][:, 2:PACK, :], halves[:, 2:PACK, :])
         load_w(2)
-        nc.sync.dma_start(bq_t[:], bq.rearrange("(p t) -> p t", t=PACK))
-        nc.sync.dma_start(pw_t, pw.rearrange("(b p t) -> p b t", b=M_PASSES, t=PACK))
         load_words(t_words[1], tab_words, 1)
         load_words(t_words[2], tab_words, 2)
         load_words(t2_words, tab2_words, 0)
@@ -163,6 +163,10 @@ def tile_list_prior_art_expansion_kernel(
         nc.vector.tensor_copy(v2_picked_scales[:], t2_scales[:].indirect(list2[:]))
         w_quantize(1)
         deal(v2_scales[:], v2_picked_scales[:], write_in_order)
+        for q in range(QUADS):
+            nc.sync.dma_start(
+                v2_scales[32 * q : 32 * q + 4, :].bitcast(I32), v2_scales[ASIDE + 4 * q : ASIDE + 4 * q + 4, :].bitcast(I32)
+            )
         w_quantize(2)
         gather_words(1, 0, S // 2)
         gather_words(1, S // 2, S)

@@ -36,6 +36,7 @@ X_BANKS = ((4, 5), (0, 1), (4, 5), (0, 1), (2, 3))
 GPSIMD_CLAIMS = (176, 0, 128, 128, 128)
 SCALAR_CLAIMS = (0, 0, 96, 128, 128)
 ASIDE = 16
+REUSED = {"vm_codes": 0, "v2_picked_scales": 2048 - 128, "vm_planes": 2048}
 OVERLAP = 32
 
 
@@ -47,7 +48,11 @@ def tile_list_prior_art_expansion_kernel(
         keep = ctx.enter_context(tc.tile_pool(name="keep", bufs=1))
         psum = ctx.enter_context(tc.psum_pool(name="psum", bufs=1))
 
+        reuse = ctx.enter_context(tc.tile_pool(name="reuse", bufs=1))
+
         def sb(name, shape, dtype):
+            if name in REUSED:
+                return reuse.tile(shape, dtype, name=name, offset=REUSED[name], align_bytes=64)
             return keep.tile(shape, dtype, name=name, align_bytes=64)
 
         def bank(k, name):
@@ -60,10 +65,8 @@ def tile_list_prior_art_expansion_kernel(
         t_words = [sb("t_words%d" % a, [P, T], I32) for a in range(K_PASSES)]
         t_scales = sb("t_scales", [P, T], U8)
         w_raw = [sb("w_raw%d" % a, [P, PACK, H], F32) for a in range(K_PASSES)]
-        vm_codes = sb("vm_codes", [P, M_PASSES * H * 2], U8)
-        vm_planes = sb("vm_planes", [P, M_PASSES * H], U8)
-        bq_t = sb("bq_t", [P, PACK], F32)
         rg_t = sb("rg_t", [P, PACK], F32)
+        bq_t = sb("bq_t", [P, PACK], F32)
         pw_pad = sb("pw_pad", [P, P], F32)
         pw_t = pw_pad[:, 0 : M_PASSES * PACK].rearrange("p (b t) -> p b t", t=PACK)
         ident = sb("ident", [P, P], F32)
@@ -71,7 +74,6 @@ def tile_list_prior_art_expansion_kernel(
 
         nc.gpsimd.memset(t2_scales[:].bitcast(I32), 0)
         nc.vector.memset(t_scales[:].bitcast(I32), 0)
-        nc.gpsimd.memset(vm_planes[:].bitcast(I32), 0)
         nc.gpsimd.memset(pw_pad[:], 0.0)
         nc.gpsimd.memset(warm[:, 0:1], 0.0)
         nc.scalar.activation(warm[:, 1:2], warm[:, 0:1], ACT.Sigmoid)
@@ -96,14 +98,6 @@ def tile_list_prior_art_expansion_kernel(
         load_words(t_words[1], tab_words, 1)
         load_words(t_words[2], tab_words, 2)
         load_words(t2_words, tab2_words, 0)
-        nc.sync.dma_start(
-            vm_codes[:].bitcast(I32).rearrange("p (b n) -> p b n", b=M_PASSES), vm_words.rearrange("b p n -> p b n").bitcast(I32)
-        )
-        for r in range(PACK):
-            nc.sync.dma_start(
-                vm_planes[r:P:32, :].bitcast(I32).rearrange("q (b n) -> q b n", b=M_PASSES),
-                vm_scales[:, r:16:4, :].rearrange("b q n -> q b n").bitcast(I32),
-            )
         with nc.allow_non_contiguous_dma(reason="one gain for each partition and output"):
             nc.sync.dma_start(rg_t[:], rg.rearrange("(t p) -> p t", t=PACK))
         for q in range(QUADS):
@@ -129,14 +123,12 @@ def tile_list_prior_art_expansion_kernel(
         write_in_order = "p b t m"
 
         v2_picked_scales = sb("v2_picked_scales", [P, S2], U8)
-        v2_codes = {}
+        v2_codes = sb("v2_codes", [P, S2], U32)
         v2_scales = sb("v2_scales", [P, S2], U8)
 
-        def gather_patents(b):
-            entries = list2[:, b * KP // LIST_ROWS : (b + 1) * KP // LIST_ROWS]
-            v2_codes[b] = sb("v2_codes%d" % b, [P, KP], U32)
-            dealt = v2_codes[b][:].rearrange("p (t m) -> p m t", t=PACK)
-            nc.vector.tensor_copy(dealt, t2_words[:].bitcast(U32).indirect(entries))
+        def gather_patents():
+            dealt = v2_codes[:].rearrange("p (b t m) -> p b m t", t=PACK, m=P)
+            nc.vector.tensor_copy(dealt, t2_words[:].bitcast(U32).indirect(list2[:]))
 
         v_codes = [sb("v_codes%d" % a, [P, S], U32) for a in range(K_PASSES)]
         v_scales = sb("v_scales", [P, S], U8)
@@ -166,6 +158,17 @@ def tile_list_prior_art_expansion_kernel(
         for q in range(QUADS):
             nc.sync.dma_start(
                 v2_scales[32 * q : 32 * q + 4, :].bitcast(I32), v2_scales[ASIDE + 4 * q : ASIDE + 4 * q + 4, :].bitcast(I32)
+            )
+        vm_codes = sb("vm_codes", [P, M_PASSES * H * 2], U8)
+        vm_planes = sb("vm_planes", [P, M_PASSES * H], U8)
+        nc.gpsimd.memset(vm_planes[:].bitcast(I32), 0)
+        nc.sync.dma_start(
+            vm_codes[:].bitcast(I32).rearrange("p (b n) -> p b n", b=M_PASSES), vm_words.rearrange("b p n -> p b n").bitcast(I32)
+        )
+        for r in range(PACK):
+            nc.sync.dma_start(
+                vm_planes[r:P:32, :].bitcast(I32).rearrange("q (b n) -> q b n", b=M_PASSES),
+                vm_scales[:, r:16:4, :].rearrange("b q n -> q b n").bitcast(I32),
             )
         w_quantize(2)
         gather_words(1, 0, S // 2)
@@ -244,7 +247,7 @@ def tile_list_prior_art_expansion_kernel(
                     m = slice(b * KP + t * P, b * KP + (t + 1) * P)
                     nc.tensor.matmul_mx(
                         e[:, t * SUB : (t + 1) * SUB],
-                        lhsT=v2_codes[b][:, t * P : (t + 1) * P].bitcast(FP8X4),
+                        lhsT=v2_codes[:, m].bitcast(FP8X4),
                         lhsT_scale=v2_scales[:, m],
                         rhs=h_codes[:, j0 : j0 + SUB].bitcast(FP8X4),
                         rhs_scale=h_scales[j0 // H_WIDTH][:, j0 % H_WIDTH : j0 % H_WIDTH + SUB],
@@ -355,8 +358,7 @@ def tile_list_prior_art_expansion_kernel(
             for a in range(K_PASSES):
                 first_product(groups - 1, half, a)
         h_round(0)
-        gather_patents(0)
-        gather_patents(1)
+        gather_patents()
         h_quantize(0)
         for g in range(1, groups):
             h_out(g)

@@ -349,8 +349,8 @@ def tile_list_prior_art_expansion_kernel(
         for a in range(K_PASSES - 1):
             for g, half in early:
                 first_product(g, half, a)
-        gather_words(K_PASSES - 1, 0, S // 2)
-        gather_words(K_PASSES - 1, S // 2, S)
+        for j0, j1 in ((0, H_WIDTH), (H_WIDTH, S // 2), (S // 2, S)):
+            gather_words(K_PASSES - 1, j0, j1)
         for g, half in early:
             first_product(g, half, K_PASSES - 1)
         h_out(0)

from contextlib import ExitStack

import concourse.mybir as mybir
from concourse.masks import make_identity

K, H, T, S, T2, S2 = 1536, 512, 4096, 1024, 2048, 1024
FLOPS = 2 * S * (K * H + H * S2 + S2 * H)

F32 = mybir.dt.float32
BF16 = mybir.dt.bfloat16
I32 = mybir.dt.int32
U32 = mybir.dt.uint32
U16 = mybir.dt.uint16
U8 = mybir.dt.uint8
FP8X4 = mybir.dt.float8_e4m3fn_x4
FP4X4 = mybir.dt.float4_e2m1fn_x4
ACT = mybir.ActivationFunctionType
ALU = mybir.AluOpType

P = 128
PACK = 4
KP = P * PACK
K_PASSES = K // KP
M_PASSES = S2 // KP
QUADS = 4
LIST_ROWS = 16
SUB = P
V_SCALE_ROW = 4

H_WIDTH = 256
H_BANKS = ((0, 1), (2, 3), (4, 5), (0, 1))
E_BANKS = (6, 2, 3)
PW_BANK = 7
WIDTHS = (256, 256, 256, 128, 128)
X_BANKS = ((4, 5), (0, 1), (4, 5), (0, 1), (2, 3))
GPSIMD_CLAIMS = (176, 0, 128, 128, 128)
SCALAR_CLAIMS = (0, 0, 96, 128, 128)
ASIDE = 16
REUSED = {"vm_codes": 0, "v2_picked_scales": 2048 - 128, "vm_planes": 2048}
OVERLAP = 32


def tile_list_prior_art_expansion_kernel(
    tc, tab_words, tab_scales, offs, tab2_words, tab2_scales, offs2, wq, bq, pw, vm_words, vm_scales, rg, out
):
    nc = tc.nc
    with ExitStack() as ctx:
        keep = ctx.enter_context(tc.tile_pool(name="keep", bufs=1))
        psum = ctx.enter_context(tc.psum_pool(name="psum", bufs=1))

        reuse = ctx.enter_context(tc.tile_pool(name="reuse", bufs=1))

        def sb(name, shape, dtype):
            if name in REUSED:
                return reuse.tile(shape, dtype, name=name, offset=REUSED[name], align_bytes=64)
            return keep.tile(shape, dtype, name=name, align_bytes=64)

        def bank(k, name):
            return psum.tile([P, KP], F32, name=name, tag="bank%d" % k)

        list1 = keep.tile([P, S // LIST_ROWS], U16, name="list1")
        list2 = keep.tile([P, S2 // LIST_ROWS], U16, name="list2")
        t2_words = sb("t2_words", [P, T2], I32)
        t2_scales = sb("t2_scales", [P, T2], U8)
        t_words = [sb("t_words%d" % a, [P, T], I32) for a in range(K_PASSES)]
        t_scales = sb("t_scales", [P, T], U8)
        w_raw = [sb("w_raw%d" % a, [P, PACK, H], F32) for a in range(K_PASSES)]
        rg_t = sb("rg_t", [P, PACK], F32)
        bq_t = sb("bq_t", [P, PACK], F32)
        pw_pad = sb("pw_pad", [P, P], F32)
        pw_t = pw_pad[:, 0 : M_PASSES * PACK].rearrange("p (b t) -> p b t", t=PACK)
        ident = sb("ident", [P, P], F32)
        warm = sb("warm", [P, 2], F32)

        nc.gpsimd.memset(t2_scales[:].bitcast(I32), 0)
        nc.vector.memset(t_scales[:].bitcast(I32), 0)
        nc.gpsimd.memset(pw_pad[:], 0.0)
        nc.gpsimd.memset(warm[:, 0:1], 0.0)
        nc.scalar.activation(warm[:, 1:2], warm[:, 0:1], ACT.Sigmoid)

        def load_words(dst, src, a):
            nc.sync.dma_start(dst[:], src[a].rearrange("p n i -> p (n i)").bitcast(I32))

        def load_w(a):
            nc.sync.dma_start(w_raw[a][:], wq[a * KP : (a + 1) * KP, :].rearrange("(p i) r -> p i r", i=PACK))

        nc.sync.dma_start(list1[:], offs)
        load_words(t_words[0], tab_words, 0)
        load_w(0)
        nc.sync.dma_start(list2[:], offs2)
        nc.sync.dma_start(t2_scales[ASIDE : 2 * ASIDE, :].bitcast(I32), tab2_scales[0].bitcast(I32))
        nc.sync.dma_start(bq_t[:], bq.rearrange("(p t) -> p t", t=PACK))
        nc.sync.dma_start(pw_t, pw.rearrange("(b p t) -> p b t", b=M_PASSES, t=PACK))
        halves = wq[KP : 2 * KP, :].rearrange("(p i) r -> p i r", i=PACK)
        nc.sync.dma_start(w_raw[1][:, 0:2, :], halves[:, 0:2, :])
        nc.sync.dma_start(w_raw[1][:, 2:PACK, :], halves[:, 2:PACK, :])
        load_w(2)
        load_words(t_words[1], tab_words, 1)
        load_words(t_words[2], tab_words, 2)
        load_words(t2_words, tab2_words, 0)
        with nc.allow_non_contiguous_dma(reason="one gain for each partition and output"):
            nc.sync.dma_start(rg_t[:], rg.rearrange("(t p) -> p t", t=PACK))
        for q in range(QUADS):
            first = 32 * q + V_SCALE_ROW
            nc.gpsimd.dma_start(
                t_scales[first : first + 4 * K_PASSES, :].bitcast(I32), tab_scales[:, 4 * q : 4 * q + 4, :].bitcast(I32)
            )

        make_identity(nc, ident[:])
        pw_bank = bank(PW_BANK, "pw_bank")
        pw_turned = sb("pw_turned", [P, P], F32)
        nc.tensor.transpose(pw_bank[:, P : 2 * P], pw_pad[:], ident[:])
        nc.scalar.copy(pw_turned[:], pw_bank[:, P : 2 * P])
        nc.tensor.transpose(pw_bank[:, 0:P], pw_turned[:], ident[:])
        pw_psum = pw_bank[:, 0 : M_PASSES * PACK].rearrange("p (b t) -> p b t", t=PACK)

        def deal(dst, src, walk):
            nc.vector.tensor_copy(
                dst.rearrange("p (b t m) -> " + walk, m=P, t=PACK),
                src.rearrange("p (b m t) -> " + walk, m=P, t=PACK),
            )

        write_in_order = "p b t m"

        v2_picked_scales = sb("v2_picked_scales", [P, S2], U8)
        v2_codes = sb("v2_codes", [P, S2], U32)
        v2_scales = sb("v2_scales", [P, S2], U8)

        def gather_patents():
            dealt = v2_codes[:].rearrange("p (b t m) -> p b m t", t=PACK, m=P)
            nc.vector.tensor_copy(dealt, t2_words[:].bitcast(U32).indirect(list2[:]))

        v_codes = [sb("v_codes%d" % a, [P, S], U32) for a in range(K_PASSES)]
        v_scales = sb("v_scales", [P, S], U8)

        def gather_words(a, j0, j1):
            entries = list1[:, j0 // LIST_ROWS : j1 // LIST_ROWS]
            nc.vector.tensor_copy(v_codes[a][:, j0:j1], t_words[a][:].bitcast(U32).indirect(entries))

        w_bf = [sb("w_bf%d" % a, [P, H * PACK], BF16) for a in range(K_PASSES)]
        w_codes = [sb("w_codes%d" % a, [P, H], U32) for a in range(K_PASSES)]
        w_scales = [sb("w_scales%d" % a, [P, H], U8) for a in range(K_PASSES)]
        for a in range(K_PASSES):
            nc.scalar.copy(
                w_bf[a][:].rearrange("p (t m i) -> p m t i", t=PACK, i=PACK),
                w_raw[a][:].rearrange("p i (m t) -> p m t i", t=PACK),
            )

        def w_quantize(a):
            nc.vector.quantize_mx(w_codes[a][:].bitcast(FP8X4), w_scales[a][:], w_bf[a][:])

        gather_words(0, 0, S)
        nc.vector.tensor_copy(v_scales[:], t_scales[:].indirect(list1[:]))
        w_quantize(0)
        nc.vector.tensor_copy(v2_picked_scales[:], t2_scales[:].indirect(list2[:]))
        w_quantize(1)
        deal(v2_scales[:], v2_picked_scales[:], write_in_order)
        for q in range(QUADS):
            nc.sync.dma_start(
                v2_scales[32 * q : 32 * q + 4, :].bitcast(I32), v2_scales[ASIDE + 4 * q : ASIDE + 4 * q + 4, :].bitcast(I32)
            )
        vm_codes = sb("vm_codes", [P, M_PASSES * H * 2], U8)
        vm_planes = sb("vm_planes", [P, M_PASSES * H], U8)
        nc.gpsimd.memset(vm_planes[:].bitcast(I32), 0)
        nc.sync.dma_start(
            vm_codes[:].bitcast(I32).rearrange("p (b n) -> p b n", b=M_PASSES), vm_words.rearrange("b p n -> p b n").bitcast(I32)
        )
        for r in range(PACK):
            nc.sync.dma_start(
                vm_planes[r:P:32, :].bitcast(I32).rearrange("q (b n) -> q b n", b=M_PASSES),
                vm_scales[:, r:16:4, :].rearrange("b q n -> q b n").bitcast(I32),
            )
        w_quantize(2)
        gather_words(1, 0, S // 2)
        gather_words(1, S // 2, S)

        chunks = len(WIDTHS)
        starts = [sum(WIDTHS[:c]) for c in range(chunks)]
        groups = S // H_WIDTH
        h_psum = {}

        def first_product(g, half, a):
            cols = slice(g * H_WIDTH, (g + 1) * H_WIDTH)
            if a == 0:
                h_psum[g, half] = bank(H_BANKS[g][half], "h%d_%d" % (g, half))
            for i in range(2):
                t = 2 * half + i
                nc.tensor.matmul_mx(
                    h_psum[g, half][:, i * H_WIDTH : (i + 1) * H_WIDTH],
                    lhsT=w_codes[a][:, t * P : (t + 1) * P].bitcast(FP8X4),
                    lhsT_scale=w_scales[a][:, t * P : (t + 1) * P],
                    rhs=v_codes[a][:, cols].bitcast(FP8X4),
                    rhs_scale=v_scales[V_SCALE_ROW + 4 * a : P, cols],
                    start=(a == 0 and i == 0),
                    stop=(a == K_PASSES - 1 and i == 1),
                )

        h = [sb("h%d" % g, [P, PACK, H_WIDTH], F32) for g in range(groups)]
        kept_h = [sb("kept_h%d" % g, [P, PACK, H_WIDTH], F32) for g in range(groups)]
        h_codes = sb("h_codes", [P, S], U32)
        h_scales = [sb("h_scales%d" % g, [P, H_WIDTH], U8) for g in range(groups)]

        d_at = []
        end = [PACK * H_WIDTH, 0]
        for c, w in enumerate(WIDTHS):
            d_at.append(end[c % 2] - (OVERLAP if GPSIMD_CLAIMS[c] else 0))
            end[c % 2] = d_at[c] + M_PASSES * PACK * w
        rounded = [sb("rounded%d" % k, [P, end[k]], BF16) for k in range(2)]
        staged = rounded[0]
        h_bf = [
            staged[:, 0 : PACK * H_WIDTH] if g == groups - 2 else sb("h_bf%d" % g, [P, H_WIDTH * PACK], BF16)[:]
            for g in range(groups)
        ]

        def h_out(g):
            for t in range(PACK):
                summed = h_psum[g, t // 2][:, (t % 2) * H_WIDTH : (t % 2 + 1) * H_WIDTH]
                if g == groups - 1:
                    nc.vector.tensor_scalar_add(h[g][:, t, :], summed, bq_t[:, t : t + 1])
                else:
                    nc.scalar.activation(h[g][:, t, :], summed, ACT.Identity, bias=bq_t[:, t : t + 1])

        def h_keep(g):
            for q in range(QUADS):
                nc.sync.dma_start(kept_h[g][:, q, :], h[g][32 * q : 32 * (q + 1), :, :])

        def h_round(g):
            copy = nc.scalar.copy if g == 0 else nc.vector.tensor_copy
            copy(
                h_bf[g].rearrange("p (n i t) -> p n t i", i=PACK, t=PACK), h[g][:].rearrange("p t (n i) -> p n t i", i=PACK)
            )

        def h_quantize(g):
            nc.vector.quantize_mx(h_codes[:, g * H_WIDTH : (g + 1) * H_WIDTH].bitcast(FP8X4), h_scales[g][:], h_bf[g])

        gate = {}
        d_codes = [sb("d_codes%d" % c, [P, M_PASSES * w], U32) for c, w in enumerate(WIDTHS)]
        d_scales = [sb("d_scales%d" % c, [P, M_PASSES * w], U8) for c, w in enumerate(WIDTHS)]

        def second_product(c, b):
            gate[c, b] = sb("gate%d_%d" % (c, b), [P, WIDTHS[c] * PACK], F32)
            for u in range(WIDTHS[c] // SUB):
                j0 = starts[c] + u * SUB
                turn = (M_PASSES * starts[c] + b * WIDTHS[c]) // SUB + u
                e = bank(E_BANKS[turn % len(E_BANKS)], "e%d" % turn)
                for t in range(PACK):
                    m = slice(b * KP + t * P, b * KP + (t + 1) * P)
                    nc.tensor.matmul_mx(
                        e[:, t * SUB : (t + 1) * SUB],
                        lhsT=v2_codes[:, m].bitcast(FP8X4),
                        lhsT_scale=v2_scales[:, m],
                        rhs=h_codes[:, j0 : j0 + SUB].bitcast(FP8X4),
                        rhs_scale=h_scales[j0 // H_WIDTH][:, j0 % H_WIDTH : j0 % H_WIDTH + SUB],
                        start=True,
                        stop=True,
                    )
                rows = SCALAR_CLAIMS[c] if b == M_PASSES - 1 and u == WIDTHS[c] // SUB - 1 else 0
                woven = SUB - rows
                by_t = e[:].rearrange("p (t n) -> p t n", t=PACK)
                if woven:
                    nc.scalar.activation(
                        gate[c, b][:, u * KP : u * KP + woven * PACK].rearrange("p (n t) -> p n t", t=PACK),
                        by_t[:, :, 0:woven].rearrange("p t n -> p n t"),
                        ACT.Sigmoid,
                    )
                if rows:
                    nc.scalar.activation(
                        gate[c, b][:, u * KP + woven * PACK : (u + 1) * KP].rearrange("p (t n) -> p t n", t=PACK),
                        by_t[:, :, woven:SUB],
                        ACT.Sigmoid,
                    )

        def d_bf(c, b, n0, n1):
            first = d_at[c] + b * WIDTHS[c] * PACK
            return rounded[c % 2][:, first + n0 * PACK : first + n1 * PACK]

        def weigh_claims(engine, weights, c, b, n0, n1):
            engine.tensor_tensor(
                d_bf(c, b, n0, n1).rearrange("p (n t) -> p n t", t=PACK),
                gate[c, b][:, n0 * PACK : n1 * PACK].rearrange("p (n t) -> p n t", t=PACK),
                weights[:, b, :].unsqueeze(1).to_broadcast([P, n1 - n0, PACK]),
                ALU.mult,
            )

        def weigh_on_scalar(c, b):
            w, n = WIDTHS[c], SCALAR_CLAIMS[c]
            rows = sb("d_rows%d_%d" % (c, b), [P, PACK, n], BF16)
            by_t = gate[c, b][:, (w - n) * PACK :].rearrange("p (t n) -> p t n", t=PACK)
            for t in range(PACK):
                nc.scalar.activation(rows[:, t, :], by_t[:, t, :], ACT.Copy, scale=pw_t[:, b, t : t + 1])
            nc.scalar.copy(
                d_bf(c, b, w - n, w).rearrange("p (n i t) -> p n t i", i=PACK, t=PACK),
                rows[:].rearrange("p t (n i) -> p n t i", i=PACK),
            )

        def weigh(c, b):
            first = GPSIMD_CLAIMS[c] if b == 0 else 0
            last = WIDTHS[c] - (SCALAR_CLAIMS[c] if b == M_PASSES - 1 else 0)
            if first:
                weigh_claims(nc.gpsimd, pw_t, c, b, 0, first)
            if first < last:
                weigh_claims(nc.vector, pw_psum, c, b, first, last)

        def d_quantize(c, b0, b1):
            w = WIDTHS[c]
            cols = slice(b0 * w, b1 * w)
            nc.vector.quantize_mx(
                d_codes[c][:, cols].bitcast(FP8X4), d_scales[c][:, cols], rounded[c % 2][:, d_at[c] + b0 * PACK * w : d_at[c] + b1 * PACK * w]
            )

        x_psum = {}

        def third_product(c, passes):
            w = WIDTHS[c]
            for half in range(2):
                for b in passes:
                    if b == 0:
                        x_psum[c, half] = bank(X_BANKS[c][half], "x%d_%d" % (c, half))
                    for i in range(2):
                        n0 = b * H + (2 * half + i) * P
                        for u in range(w // SUB):
                            cols = slice(b * w + u * SUB, b * w + (u + 1) * SUB)
                            nc.tensor.matmul_mx(
                                x_psum[c, half][:, i * w + u * SUB : i * w + (u + 1) * SUB],
                                lhsT=vm_codes[:, 2 * n0 : 2 * (n0 + P)].bitcast(FP4X4),
                                lhsT_scale=vm_planes[:, n0 : n0 + P],
                                rhs=d_codes[c][:, cols].bitcast(FP8X4),
                                rhs_scale=d_scales[c][:, cols],
                                start=(b == 0 and i == 0 and u == 0),
                                stop=(b == M_PASSES - 1 and i == 1 and u == w // SUB - 1),
                            )

        out_rows = out.rearrange("(t p) j -> p t j", t=PACK)

        def finish(c):
            w = WIDTHS[c]
            g, j0 = divmod(starts[c], H_WIDTH)
            for half in range(2):
                for i in range(2):
                    t = 2 * half + i
                    kept = kept_h[g][:, t, j0 : j0 + w]
                    nc.vector.scalar_tensor_tensor(
                        kept, kept, rg_t[:, t : t + 1], x_psum[c, half][:, i * w : (i + 1) * w], ALU.mult, ALU.add
                    )
                ts = slice(2 * half, 2 * half + 2)
                nc.sync.dma_start(out_rows[:, ts, starts[c] : starts[c] + w], kept_h[g][:, ts, j0 : j0 + w])

        early = [(g, half) for g in range(groups - 1) for half in range(2)]
        for a in range(K_PASSES - 1):
            for g, half in early:
                first_product(g, half, a)
        for j0, j1 in ((0, H_WIDTH), (H_WIDTH, S // 2), (S // 2, S)):
            gather_words(K_PASSES - 1, j0, j1)
        for g, half in early:
            first_product(g, half, K_PASSES - 1)
        h_out(0)
        for half in range(2):
            for a in range(K_PASSES):
                first_product(groups - 1, half, a)
        h_round(0)
        gather_patents()
        h_quantize(0)
        for g in range(1, groups):
            h_out(g)
        for g in range(groups):
            h_keep(g)
        h_round(1)
        h_round(3)
        h_quantize(1)
        h_round(2)
        h_quantize(3)
        h_quantize(2)
        for c in range(chunks):
            for b in range(M_PASSES):
                second_product(c, b)
                if (c, b) == (3, 0):
                    weigh_on_scalar(2, 1)
        weigh_on_scalar(3, 1)
        weigh_on_scalar(4, 1)
        last = chunks - 1
        for c in range(last):
            for b in range(M_PASSES):
                weigh(c, b)
            d_quantize(c, 0, M_PASSES)
            if c > 0:
                finish(c - 1)
            third_product(c, range(M_PASSES))
        for b in range(M_PASSES):
            weigh(last, b)
            d_quantize(last, b, b + 1)
            third_product(last, [b])
        finish(last - 1)
        finish(last)
